import numpy as np
import ml_dtypes


def mxq(x, axis, fmt="e4m3"):
    dtype, down = {"e4m3": (ml_dtypes.float8_e4m3fn, 7), "e5m2": (ml_dtypes.float8_e5m2, 14)}[fmt]
    v = np.moveaxis(np.asarray(x, np.float32).astype(ml_dtypes.bfloat16).astype(np.float64), axis, -1)
    blocks = v.reshape(v.shape[:-1] + (-1, 32))
    amax = np.abs(blocks).max(-1, keepdims=True)
    byte = np.maximum(np.where(amax > 0, np.frexp(amax)[1] - 1 + 127, 0) - down, 1)
    scale = np.exp2(byte - 127.0)
    codes = (blocks / scale).astype(np.float32).astype(dtype).astype(np.float64)
    return np.moveaxis((codes * scale).reshape(v.shape), -1, axis)


WIDE = False


def mx_kscale(k):
    if not WIDE:
        return np.ones(k)
    levels = np.array([10, -10, 5, -5, 0])
    if k % 512:
        return np.exp2(np.random.permutation(np.resize(levels, k // 32))).repeat(32)
    a = np.empty((k // 512, 16))
    for p in range(k // 512):
        a[p, :8] = np.random.permutation(np.resize(levels, 8))
        for g in range(8):
            far = levels[np.abs(levels - a[p, g]) >= 10]
            a[p, g + 8] = far[np.random.randint(len(far))]
    return np.exp2(a.ravel()).repeat(32)


def f64(x):
    return np.asarray(x).astype(np.float64)


def striped(idx):
    return np.tile(idx.reshape(-1, 16).T, (8, 1)).astype(np.uint16)


def unstriped(offs):
    return offs[:16].T.reshape(-1).astype(np.int64)


def pack_weight(w):
    k, n = w.shape
    w = f64(np.asarray(w, np.float32).astype(ml_dtypes.bfloat16)).reshape(k // 32, 32, n)
    amax = np.abs(w).max(1)
    byte = np.clip(np.where(amax > 0, np.frexp(amax)[1] - 1 + 127 - 7, 1), 1, 254)
    scaled = (w * np.exp2(127.0 - byte)[:, None, :]).reshape(k, n).astype(np.float32)
    words = np.ascontiguousarray(scaled.reshape(k // 512, 128, 4, n).transpose(0, 1, 3, 2)).astype(ml_dtypes.float8_e4m3fn).view(np.uint8)
    return words, np.ascontiguousarray(byte.astype(np.uint8).reshape(k // 512, 16, n))


def unpack_weight(words, scales):
    g, p, n, _ = words.shape
    vals = np.ascontiguousarray(words).view(ml_dtypes.float8_e4m3fn).astype(np.float64) * np.repeat(np.exp2(scales.astype(np.float64) - 127.0), 8, axis=1)[..., None]
    return vals.transpose(0, 1, 3, 2).reshape(g * 512, n)


def planes(y):
    n, m = y.shape
    v = y.astype(np.float32).astype(ml_dtypes.bfloat16).astype(np.float64).reshape(n // 32, 32, m)
    top = np.abs(v).max(1)
    byte = np.clip(np.where(top > 0, np.frexp(top)[1] - 1 + 127 - 7, 1), 1, 254)
    codes = (v * np.exp2(127.0 - byte)[:, None, :]).reshape(n, m).astype(np.float32).astype(ml_dtypes.float8_e4m3fn).view(np.uint8)
    words = codes.reshape(n // 512, 128, 4, m).transpose(0, 1, 3, 2)
    return np.ascontiguousarray(words), np.ascontiguousarray(byte.astype(np.uint8).reshape(n // 512, 16, m))


K, T, S, V, H, N = 512, 4096, 1024, 256, 512, 512


def setup_inputs():
    n = np.random.standard_normal
    s = mx_kscale(K)[:, None]
    u = mx_kscale(H)
    packed_xT = pack_weight(n((K, T)) * s)
    return {
        "x_words": packed_xT[0],
        "x_scales": packed_xT[1],
        "w1": (n((K, H)) / np.sqrt(K) / s * u).astype(np.float32),
        "w2": (n((K, N)) / np.sqrt(K) / s).astype(np.float32),
        "w3": (n((H, N)) / np.sqrt(H) / u[:, None]).astype(np.float32),
        "offs": striped(np.random.permutation(T)[:S]),
    }


def reference(x_words, x_scales, w1, w2, w3, offs):
    xq = unpack_weight(x_words, x_scales)[:, unstriped(offs)]
    w1q = mxq(f64(w1), 0, "e4m3")
    h0 = w1q.T @ xq[:, :V]
    w2q = mxq(f64(w2), 0, "e4m3")
    e1 = w2q.T @ xq[:, V:2 * V]
    e2 = w2q.T @ xq[:, 2 * V:3 * V]
    e3 = w2q.T @ xq[:, 3 * V:4 * V]
    h1 = w1q.T @ xq[:, V:2 * V]
    h2 = w1q.T @ xq[:, 2 * V:3 * V]
    z = h0 * e1 + h0 * e2 + h0 * e3 + h1 * e2 + h1 * e3 + h2 * e3
    out_0 = mxq(f64(w3), 0, "e4m3").T @ mxq(z, 0, "e4m3")
    return (out_0,) + planes(out_0)

@@ -1,0 +1,196 @@
+from contextlib import ExitStack
+
+import concourse.mybir as mybir
+from concourse.masks import make_identity
+
+K, T, S, V, H, N = 512, 4096, 1024, 256, 512, 512
+FLOPS = 7 * 2 * K * H * V
+
+F32 = mybir.dt.float32
+BF16 = mybir.dt.bfloat16
+I32 = mybir.dt.int32
+U32 = mybir.dt.uint32
+U16 = mybir.dt.uint16
+U8 = mybir.dt.uint8
+FP8X4 = mybir.dt.float8_e4m3fn_x4
+MULT = mybir.AluOpType.mult
+ADD = mybir.AluOpType.add
+
+P = 128
+PACK = 4
+HALF = H // 2
+BLOCKS = V // P
+FIRST = 1024
+
+
+def tile_picked_zfibi_none_po_kernel(
+    tc, x_words, x_scales, w1, w2, w3, offs, out_0, out_1, out_2
+):
+    nc = tc.nc
+    with ExitStack() as ctx:
+        keep = ctx.enter_context(tc.tile_pool(name="keep", bufs=1))
+        psum = ctx.enter_context(tc.psum_pool(name="psum", bufs=8))
+
+        offsets = keep.tile([P, S // 16], U16, name="offsets")
+        nc.sync.dma_start(offsets[:], offs)
+
+        scale_table = keep.tile([P, T], U8, name="scale_table", align_bytes=64)
+        nc.vector.memset(scale_table[:].bitcast(I32), 0)
+        word_table = keep.tile([P, T], U32, name="word_table", align_bytes=64)
+        word_rows = x_words[0].rearrange("p n t -> p (n t)").bitcast(I32)
+        nc.sync.dma_start(word_table[:, :FIRST].bitcast(I32), word_rows[:, :FIRST])
+        for q in range(4):
+            nc.sync.dma_start(
+                scale_table[32 * q : 32 * q + 4, :].bitcast(I32), x_scales[0, 4 * q : 4 * q + 4, :].bitcast(I32)
+            )
+        nc.sync.dma_start(word_table[:, FIRST:].bitcast(I32), word_rows[:, FIRST:])
+
+        def load(name, weight, half):
+            raw = keep.tile([P, PACK, HALF], F32, name=name, align_bytes=64)
+            rows = weight.rearrange("(p j) c -> p j c", j=PACK)
+            nc.sync.dma_start(raw[:], rows[:, :, half * HALF : (half + 1) * HALF])
+            return raw
+
+        w1_raw, w2_raw, w3_raw = [], [], []
+        for half in range(2):
+            w1_raw.append(load(f"w1_raw{half}", w1, half))
+            w2_raw.append(load(f"w2_raw{half}", w2, half))
+        for half in range(2):
+            w3_raw.append(load(f"w3_raw{half}", w3, half))
+
+        identity = keep.tile([P, P], F32, name="identity", align_bytes=64)
+        make_identity(nc, identity[:])
+
+        x_scale = keep.tile([P, S], U8, name="x_scale", align_bytes=64)
+        nc.vector.tensor_copy(x_scale[:], scale_table[:].indirect(offsets[:]))
+        x_code = []
+        for pair in range(2):
+            gathered = keep.tile([P, 2 * V], U32, name=f"x_code{pair}", align_bytes=64)
+            nc.vector.tensor_copy(gathered[:], word_table[:].indirect(offsets[:, 32 * pair : 32 * (pair + 1)]))
+            x_code.append(gathered)
+
+        def field(d, block):
+            first = (d % 2) * V + block * P
+            codes = x_code[d // 2][:, first : first + P].bitcast(FP8X4)
+            return codes, x_scale[:, d * V + block * P : d * V + (block + 1) * P]
+
+        def quantise(name, grouped, width):
+            codes = keep.tile([P, width], U32, name=name + "_code", align_bytes=64)
+            scales = keep.tile([P, width], U8, name=name + "_scale", align_bytes=64)
+            nc.vector.quantize_mx(out=codes[:].bitcast(FP8X4), scales=scales[:], in_=grouped)
+            return codes, scales
+
+        def group(copy, raw, tag):
+            grouped = keep.tile([P, HALF, PACK], BF16, name="grouped", tag=tag, align_bytes=64)
+            copy(grouped[:], raw[:].rearrange("p j c -> p c j"))
+            return grouped[:].rearrange("p c j -> p (c j)")
+
+        def project(fields, weight):
+            bank = psum.tile([P, BLOCKS, HALF], F32, name="bank", tag="bank")
+            for block in range(BLOCKS):
+                for n, d in enumerate(fields):
+                    codes, scales = field(d, block)
+                    nc.tensor.matmul_mx(
+                        out=bank[:, block, :],
+                        lhsT=codes,
+                        lhsT_scale=scales,
+                        rhs=weight[0][:].bitcast(FP8X4),
+                        rhs_scale=weight[1][:],
+                        start=(n == 0),
+                        stop=(n == len(fields) - 1),
+                    )
+            return bank[:].rearrange("p b (m t) -> p b t m", t=PACK)
+
+        def left_tiles(half):
+            return [keep.tile([P, BLOCKS, PACK, HALF // PACK], F32, name=f"left{k}_{half}") for k in range(3)]
+
+        product = [keep.tile([P, BLOCKS, PACK, P], F32, name=f"product{k}", align_bytes=64) for k in range(3)]
+        low, high = slice(0, P // 2), slice(P // 2, P)
+
+        w1a = quantise("w1a", group(nc.scalar.copy, w1_raw[0], "left_weights"), HALF)
+        left_banks = [project(fields, w1a) for fields in ([0], [0, 1], [2])]
+        w2a = quantise("w2a", group(nc.scalar.copy, w2_raw[0], "right_weights"), HALF)
+        left_a = left_tiles(0)
+        for k in range(3):
+            nc.scalar.copy(left_a[k][:], left_banks[k])
+        right_a = [project(fields, w2a) for fields in ([1], [2], [3])]
+        nc.gpsimd.tensor_tensor(left_a[2][:], left_a[2][:], left_a[1][:], ADD)
+        w1b = quantise("w1b", group(nc.vector.tensor_copy, w1_raw[1], "left_weights"), HALF)
+        left_banks = [project(fields, w1b) for fields in ([0], [0, 1], [2])]
+        w2b_grouped = group(nc.scalar.copy, w2_raw[1], "right_weights")
+        for k in range(3):
+            nc.vector.tensor_tensor(product[k][:, :, :, low], right_a[k], left_a[k][:], MULT)
+            if k == 2:
+                w2b = quantise("w2b", w2b_grouped, HALF)
+        left_b = left_tiles(1)
+        for k in range(3):
+            nc.scalar.copy(left_b[k][:], left_banks[k])
+        right_b = [project(fields, w2b) for fields in ([1], [2, 3], [3])]
+
+        w3_grouped = keep.tile([P, PACK, P, PACK], BF16, name="w3_grouped", tag="right_weights", align_bytes=64)
+        w3_dealt = [w3_grouped[:, :, rows, :].rearrange("p t m j -> p m t j") for rows in (low, high)]
+        w3_read = [raw[:].rearrange("p j (m t) -> p m t j", t=PACK) for raw in w3_raw]
+        nc.gpsimd.tensor_scalar(w3_dealt[0], w3_read[0], 1.0, 0.0, MULT, ADD)
+        nc.gpsimd.tensor_scalar(w3_dealt[1], w3_read[1], 1.0, 0.0, MULT, ADD)
+
+        for block in range(BLOCKS):
+            for k in range(3):
+                nc.vector.tensor_tensor(product[k][:, block, :, high], right_b[k][:, block], left_b[k][:, block], MULT)
+        w3_code, w3_scale = quantise("w3q", w3_grouped[:].rearrange("p t m j -> p (t m j)"), N)
+
+        z_grouped = []
+        for block in range(BLOCKS):
+            z_bank = psum.tile([P, PACK, P], F32, name="bank", tag="bank")
+            for k in range(3):
+                for t in range(PACK):
+                    nc.tensor.matmul(
+                        z_bank[:, t, :],
+                        product[k][:, block, t, :],
+                        identity[:],
+                        start=(k == 0 and t == 0),
+                        stop=(k == 2 and t == PACK - 1),
+                        is_transpose=True,
+                    )
+            grouped = keep.tile([P, P, PACK], BF16, name=f"z_grouped{block}", align_bytes=64)
+            nc.scalar.copy(grouped[:], z_bank[:].rearrange("p t v -> p v t"))
+            z_grouped.append(grouped)
+
+        results = []
+        for block in range(BLOCKS):
+            z_code, z_scale = quantise(f"zq{block}", z_grouped[block][:].rearrange("p v t -> p (v t)"), P)
+            out_bank = psum.tile([P, PACK, P], F32, name="bank", tag="bank")
+            for t in range(PACK):
+                nc.tensor.matmul_mx(
+                    out=out_bank[:, t, :],
+                    lhsT=w3_code[:, t * P : (t + 1) * P].bitcast(FP8X4),
+                    lhsT_scale=w3_scale[:, t * P : (t + 1) * P],
+                    rhs=z_code[:].bitcast(FP8X4),
+                    rhs_scale=z_scale[:],
+                    start=True,
+                    stop=True,
+                )
+            result = keep.tile([P, PACK, P], F32, name=f"result{block}")
+            nc.scalar.copy(result[:], out_bank[:])
+            results.append(result)
+
+        out_code = keep.tile([P, V], U32, name="out_code", align_bytes=64)
+        out_scale = keep.tile([P, V], U8, name="out_scale", align_bytes=64)
+        out_words = out_1[0].rearrange("p n t -> p (n t)").bitcast(I32)
+        out_rows = out_0.rearrange("(p t) v -> p t v", t=PACK)
+        for block in range(BLOCKS):
+            cols = slice(block * P, (block + 1) * P)
+            nc.sync.dma_start(out_rows[:, :, cols], results[block][:])
+            out_grouped = keep.tile([P, P, PACK], BF16, name=f"out_grouped{block}", align_bytes=64)
+            nc.vector.tensor_copy(out_grouped[:], results[block][:].rearrange("p t v -> p v t"))
+            nc.vector.quantize_mx(
+                out=out_code[:, cols].bitcast(FP8X4),
+                scales=out_scale[:, cols],
+                in_=out_grouped[:].rearrange("p v t -> p (v t)"),
+            )
+            nc.sync.dma_start(out_words[:, cols], out_code[:, cols].bitcast(I32))
+
+        for q in range(4):
+            queue = nc.scalar if q % 2 else nc.sync
+            queue.dma_start(
+                out_2[0, 4 * q : 4 * q + 4, :].bitcast(I32), out_scale[32 * q : 32 * q + 4, :].bitcast(I32)
+            )

@@ -18,9 +18,10 @@ ADD = mybir.AluOpType.add
 
 P = 128
 PACK = 4
+QUADRANT = 32
 HALF = H // 2
 BLOCKS = V // P
-FIRST = 1024
+LINE = 4
 
 
 def tile_picked_zfibi_none_po_kernel(
@@ -31,35 +32,47 @@ def tile_picked_zfibi_none_po_kernel(
         keep = ctx.enter_context(tc.tile_pool(name="keep", bufs=1))
         psum = ctx.enter_context(tc.psum_pool(name="psum", bufs=8))
 
-        offsets = keep.tile([P, S // 16], U16, name="offsets")
-        nc.sync.dma_start(offsets[:], offs)
-
-        scale_table = keep.tile([P, T], U8, name="scale_table", align_bytes=64)
-        nc.vector.memset(scale_table[:].bitcast(I32), 0)
-        word_table = keep.tile([P, T], U32, name="word_table", align_bytes=64)
-        word_rows = x_words[0].rearrange("p n t -> p (n t)").bitcast(I32)
-        nc.sync.dma_start(word_table[:, :FIRST].bitcast(I32), word_rows[:, :FIRST])
-        for q in range(4):
-            nc.sync.dma_start(
-                scale_table[32 * q : 32 * q + 4, :].bitcast(I32), x_scales[0, 4 * q : 4 * q + 4, :].bitcast(I32)
-            )
-        nc.sync.dma_start(word_table[:, FIRST:].bitcast(I32), word_rows[:, FIRST:])
-
         def load(name, weight, half):
             raw = keep.tile([P, PACK, HALF], F32, name=name, align_bytes=64)
             rows = weight.rearrange("(p j) c -> p j c", j=PACK)
             nc.sync.dma_start(raw[:], rows[:, :, half * HALF : (half + 1) * HALF])
             return raw
 
-        w1_raw, w2_raw, w3_raw = [], [], []
-        for half in range(2):
-            w1_raw.append(load(f"w1_raw{half}", w1, half))
-            w2_raw.append(load(f"w2_raw{half}", w2, half))
-        for half in range(2):
-            w3_raw.append(load(f"w3_raw{half}", w3, half))
+        offsets = keep.tile([P, S // 16], U16, name="offsets")
+        nc.sync.dma_start(offsets[:], offs)
+        scale_table = keep.tile([P, T], U8, name="scale_table", align_bytes=64)
+        nc.vector.memset(scale_table[:].bitcast(I32), 0)
+        w1_raw = [load("w1_raw0", w1, 0)]
+        for r in range(4):
+            nc.sync.dma_start(scale_table[r:P:QUADRANT, :].bitcast(I32), x_scales[0, r:16:4, :].bitcast(I32))
+        word_table = keep.tile([P, T], U32, name="word_table", align_bytes=64)
+        nc.sync.dma_start(word_table[:].bitcast(I32), x_words[0].rearrange("p n t -> p (n t)").bitcast(I32))
+        w2_raw = [load("w2_raw0", w2, 0)]
+        w1_raw.append(load("w1_raw1", w1, 1))
+        w2_raw.append(load("w2_raw1", w2, 1))
+        w3_raw = [load(f"w3_raw{half}", w3, half) for half in range(2)]
 
         identity = keep.tile([P, P], F32, name="identity", align_bytes=64)
         make_identity(nc, identity[:])
+
+        def interleave(copy, grouped, planes):
+            copy(
+                grouped.rearrange("p (c i) j -> p c j i", i=LINE),
+                planes.rearrange("p j (c i) -> p c j i", i=LINE),
+            )
+
+        def group(copy, raw, tag):
+            grouped = keep.tile([P, HALF, PACK], BF16, name="grouped", tag=tag, align_bytes=64)
+            interleave(copy, grouped[:], raw[:])
+            return grouped[:].rearrange("p c j -> p (c j)")
+
+        def quantise(name, grouped, width):
+            codes = keep.tile([P, width], U32, name=name + "_code", align_bytes=64)
+            scales = keep.tile([P, width], U8, name=name + "_scale", align_bytes=64)
+            nc.vector.quantize_mx(out=codes[:].bitcast(FP8X4), scales=scales[:], in_=grouped)
+            return codes, scales
+
+        w1a = quantise("w1a", group(nc.scalar.copy, w1_raw[0], "left_weights"), HALF)
 
         x_scale = keep.tile([P, S], U8, name="x_scale", align_bytes=64)
         nc.vector.tensor_copy(x_scale[:], scale_table[:].indirect(offsets[:]))
@@ -69,31 +82,15 @@ def tile_picked_zfibi_none_po_kernel(
             nc.vector.tensor_copy(gathered[:], word_table[:].indirect(offsets[:, 32 * pair : 32 * (pair + 1)]))
             x_code.append(gathered)
 
-        def field(d, block):
-            first = (d % 2) * V + block * P
-            codes = x_code[d // 2][:, first : first + P].bitcast(FP8X4)
-            return codes, x_scale[:, d * V + block * P : d * V + (block + 1) * P]
-
-        def quantise(name, grouped, width):
-            codes = keep.tile([P, width], U32, name=name + "_code", align_bytes=64)
-            scales = keep.tile([P, width], U8, name=name + "_scale", align_bytes=64)
-            nc.vector.quantize_mx(out=codes[:].bitcast(FP8X4), scales=scales[:], in_=grouped)
-            return codes, scales
-
-        def group(copy, raw, tag):
-            grouped = keep.tile([P, HALF, PACK], BF16, name="grouped", tag=tag, align_bytes=64)
-            copy(grouped[:], raw[:].rearrange("p j c -> p c j"))
-            return grouped[:].rearrange("p c j -> p (c j)")
-
         def project(fields, weight):
             bank = psum.tile([P, BLOCKS, HALF], F32, name="bank", tag="bank")
             for block in range(BLOCKS):
                 for n, d in enumerate(fields):
-                    codes, scales = field(d, block)
+                    first = d * V + block * P
                     nc.tensor.matmul_mx(
                         out=bank[:, block, :],
-                        lhsT=codes,
-                        lhsT_scale=scales,
+                        lhsT=x_code[d // 2][:, first % (2 * V) : first % (2 * V) + P].bitcast(FP8X4),
+                        lhsT_scale=x_scale[:, first : first + P],
                         rhs=weight[0][:].bitcast(FP8X4),
                         rhs_scale=weight[1][:],
                         start=(n == 0),
@@ -107,35 +104,35 @@ def tile_picked_zfibi_none_po_kernel(
         product = [keep.tile([P, BLOCKS, PACK, P], F32, name=f"product{k}", align_bytes=64) for k in range(3)]
         low, high = slice(0, P // 2), slice(P // 2, P)
 
-        w1a = quantise("w1a", group(nc.scalar.copy, w1_raw[0], "left_weights"), HALF)
         left_banks = [project(fields, w1a) for fields in ([0], [0, 1], [2])]
         w2a = quantise("w2a", group(nc.scalar.copy, w2_raw[0], "right_weights"), HALF)
         left_a = left_tiles(0)
-        for k in range(3):
+        for k in range(2):
             nc.scalar.copy(left_a[k][:], left_banks[k])
         right_a = [project(fields, w2a) for fields in ([1], [2], [3])]
-        nc.gpsimd.tensor_tensor(left_a[2][:], left_a[2][:], left_a[1][:], ADD)
-        w1b = quantise("w1b", group(nc.vector.tensor_copy, w1_raw[1], "left_weights"), HALF)
-        left_banks = [project(fields, w1b) for fields in ([0], [0, 1], [2])]
+        w1b_grouped = group(nc.vector.tensor_copy, w1_raw[1], "left_weights")
         w2b_grouped = group(nc.scalar.copy, w2_raw[1], "right_weights")
-        for k in range(3):
-            nc.vector.tensor_tensor(product[k][:, :, :, low], right_a[k], left_a[k][:], MULT)
-            if k == 2:
-                w2b = quantise("w2b", w2b_grouped, HALF)
+        nc.vector.tensor_tensor(product[0][:, :, :, low], right_a[0], left_a[0][:], MULT)
+        w1b = quantise("w1b", w1b_grouped, HALF)
+        nc.vector.tensor_tensor(left_a[2][:], left_banks[2], left_a[1][:], ADD)
+        left_banks = [project(fields, w1b) for fields in ([0], [0, 1], [2])]
+        w2b = quantise("w2b", w2b_grouped, HALF)
         left_b = left_tiles(1)
         for k in range(3):
             nc.scalar.copy(left_b[k][:], left_banks[k])
         right_b = [project(fields, w2b) for fields in ([1], [2, 3], [3])]
-
-        w3_grouped = keep.tile([P, PACK, P, PACK], BF16, name="w3_grouped", tag="right_weights", align_bytes=64)
-        w3_dealt = [w3_grouped[:, :, rows, :].rearrange("p t m j -> p m t j") for rows in (low, high)]
-        w3_read = [raw[:].rearrange("p j (m t) -> p m t j", t=PACK) for raw in w3_raw]
-        nc.gpsimd.tensor_scalar(w3_dealt[0], w3_read[0], 1.0, 0.0, MULT, ADD)
-        nc.gpsimd.tensor_scalar(w3_dealt[1], w3_read[1], 1.0, 0.0, MULT, ADD)
-
+        for k in (1, 2):
+            nc.vector.tensor_tensor(product[k][:, :, :, low], right_a[k], left_a[k][:], MULT)
         for block in range(BLOCKS):
             for k in range(3):
                 nc.vector.tensor_tensor(product[k][:, block, :, high], right_b[k][:, block], left_b[k][:, block], MULT)
+
+        w3_grouped = keep.tile([P, PACK, P, PACK], BF16, name="w3_grouped", align_bytes=64)
+        for copy, raw, rows in zip((nc.scalar.copy, nc.vector.tensor_copy), w3_raw, (low, high)):
+            copy(
+                w3_grouped[:, :, rows, :].rearrange("p t m j -> p m j t"),
+                raw[:].rearrange("p j (m t) -> p m j t", t=PACK),
+            )
         w3_code, w3_scale = quantise("w3q", w3_grouped[:].rearrange("p t m j -> p (t m j)"), N)
 
         z_grouped = []
@@ -155,7 +152,7 @@ def tile_picked_zfibi_none_po_kernel(
             nc.scalar.copy(grouped[:], z_bank[:].rearrange("p t v -> p v t"))
             z_grouped.append(grouped)
 
-        results = []
+        out_banks = []
         for block in range(BLOCKS):
             z_code, z_scale = quantise(f"zq{block}", z_grouped[block][:].rearrange("p v t -> p (v t)"), P)
             out_bank = psum.tile([P, PACK, P], F32, name="bank", tag="bank")
@@ -169,9 +166,7 @@ def tile_picked_zfibi_none_po_kernel(
                     start=True,
                     stop=True,
                 )
-            result = keep.tile([P, PACK, P], F32, name=f"result{block}")
-            nc.scalar.copy(result[:], out_bank[:])
-            results.append(result)
+            out_banks.append(out_bank)
 
         out_code = keep.tile([P, V], U32, name="out_code", align_bytes=64)
         out_scale = keep.tile([P, V], U8, name="out_scale", align_bytes=64)
@@ -179,9 +174,12 @@ def tile_picked_zfibi_none_po_kernel(
         out_rows = out_0.rearrange("(p t) v -> p t v", t=PACK)
         for block in range(BLOCKS):
             cols = slice(block * P, (block + 1) * P)
-            nc.sync.dma_start(out_rows[:, :, cols], results[block][:])
+            result = keep.tile([P, PACK, P], F32, name=f"result{block}", align_bytes=64)
             out_grouped = keep.tile([P, P, PACK], BF16, name=f"out_grouped{block}", align_bytes=64)
-            nc.vector.tensor_copy(out_grouped[:], results[block][:].rearrange("p t v -> p v t"))
+            for part in (low, high):
+                nc.scalar.copy(result[:, :, part], out_banks[block][:, :, part])
+                interleave(nc.vector.tensor_copy, out_grouped[:, part, :], result[:, :, part])
+            nc.sync.dma_start(out_rows[:, :, cols], result[:])
             nc.vector.quantize_mx(
                 out=out_code[:, cols].bitcast(FP8X4),
                 scales=out_scale[:, cols],
@@ -189,8 +187,6 @@ def tile_picked_zfibi_none_po_kernel(
             )
             nc.sync.dma_start(out_words[:, cols], out_code[:, cols].bitcast(I32))
 
-        for q in range(4):
-            queue = nc.scalar if q % 2 else nc.sync
-            queue.dma_start(
-                out_2[0, 4 * q : 4 * q + 4, :].bitcast(I32), out_scale[32 * q : 32 * q + 4, :].bitcast(I32)
-            )
+        for r in range(4):
+            queue = nc.scalar if r % 2 else nc.sync
+            queue.dma_start(out_2[0, r:16:4, :].bitcast(I32), out_scale[r:P:QUADRANT, :].bitcast(I32))

@@ -22,6 +22,7 @@ QUADRANT = 32
 HALF = H // 2
 BLOCKS = V // P
 LINE = 4
+RUN = 8
 
 
 def tile_picked_zfibi_none_po_kernel(
@@ -39,10 +40,10 @@ def tile_picked_zfibi_none_po_kernel(
             return raw
 
         offsets = keep.tile([P, S // 16], U16, name="offsets")
-        nc.sync.dma_start(offsets[:], offs)
         scale_table = keep.tile([P, T], U8, name="scale_table", align_bytes=64)
         nc.vector.memset(scale_table[:].bitcast(I32), 0)
         w1_raw = [load("w1_raw0", w1, 0)]
+        nc.sync.dma_start(offsets[:], offs)
         for r in range(4):
             nc.sync.dma_start(scale_table[r:P:QUADRANT, :].bitcast(I32), x_scales[0, r:16:4, :].bitcast(I32))
         word_table = keep.tile([P, T], U32, name="word_table", align_bytes=64)
@@ -50,7 +51,9 @@ def tile_picked_zfibi_none_po_kernel(
         w2_raw = [load("w2_raw0", w2, 0)]
         w1_raw.append(load("w1_raw1", w1, 1))
         w2_raw.append(load("w2_raw1", w2, 1))
-        w3_raw = [load(f"w3_raw{half}", w3, half) for half in range(2)]
+        w3_raw = keep.tile([P, PACK, N], F32, name="w3_raw", align_bytes=64)
+        for j in range(PACK):
+            nc.sync.dma_start(w3_raw[:, j, :], w3.rearrange("(b j q) c -> j b q c", j=PACK, q=RUN)[j])
 
         identity = keep.tile([P, P], F32, name="identity", align_bytes=64)
         make_identity(nc, identity[:])
@@ -82,57 +85,85 @@ def tile_picked_zfibi_none_po_kernel(
             nc.vector.tensor_copy(gathered[:], word_table[:].indirect(offsets[:, 32 * pair : 32 * (pair + 1)]))
             x_code.append(gathered)
 
-        def project(fields, weight):
-            bank = psum.tile([P, BLOCKS, HALF], F32, name="bank", tag="bank")
-            for block in range(BLOCKS):
-                for n, d in enumerate(fields):
-                    first = d * V + block * P
-                    nc.tensor.matmul_mx(
-                        out=bank[:, block, :],
-                        lhsT=x_code[d // 2][:, first % (2 * V) : first % (2 * V) + P].bitcast(FP8X4),
-                        lhsT_scale=x_scale[:, first : first + P],
-                        rhs=weight[0][:].bitcast(FP8X4),
-                        rhs_scale=weight[1][:],
-                        start=(n == 0),
-                        stop=(n == len(fields) - 1),
-                    )
-            return bank[:].rearrange("p b (m t) -> p b t m", t=PACK)
+        def project(out, fields, block, codes, scales):
+            for n, d in enumerate(fields):
+                first = d * V + block * P
+                nc.tensor.matmul_mx(
+                    out=out,
+                    lhsT=x_code[d // 2][:, first % (2 * V) : first % (2 * V) + P].bitcast(FP8X4),
+                    lhsT_scale=x_scale[:, first : first + P],
+                    rhs=codes.bitcast(FP8X4),
+                    rhs_scale=scales,
+                    start=(n == 0),
+                    stop=(n == len(fields) - 1),
+                )
 
-        def left_tiles(half):
-            return [keep.tile([P, BLOCKS, PACK, HALF // PACK], F32, name=f"left{k}_{half}") for k in range(3)]
+        def project_left(weight):
+            banks = []
+            for fields in ([0], [0, 1], [2]):
+                bank = psum.tile([P, BLOCKS, HALF], F32, name="bank", tag="bank")
+                for block in range(BLOCKS):
+                    project(bank[:, block, :], fields, block, weight[0][:], weight[1][:])
+                banks.append(bank)
+            return banks
 
+        left = [keep.tile([P, BLOCKS, H], F32, name=f"left{k}", align_bytes=64) for k in range(3)]
         product = [keep.tile([P, BLOCKS, PACK, P], F32, name=f"product{k}", align_bytes=64) for k in range(3)]
+        w2_code = keep.tile([P, H], U32, name="w2_code", align_bytes=64)
+        w2_scale = keep.tile([P, H], U8, name="w2_scale", align_bytes=64)
+        first_half, second_half, whole = slice(0, HALF), slice(HALF, H), slice(0, H)
         low, high = slice(0, P // 2), slice(P // 2, P)
 
-        left_banks = [project(fields, w1a) for fields in ([0], [0, 1], [2])]
-        w2a = quantise("w2a", group(nc.scalar.copy, w2_raw[0], "right_weights"), HALF)
-        left_a = left_tiles(0)
-        for k in range(2):
-            nc.scalar.copy(left_a[k][:], left_banks[k])
-        right_a = [project(fields, w2a) for fields in ([1], [2], [3])]
+        def quantise_w2(grouped, cols):
+            nc.vector.quantize_mx(out=w2_code[:, cols].bitcast(FP8X4), scales=w2_scale[:, cols], in_=grouped)
+
+        def multiply(k, block, bank, cols):
+            rows = slice(cols.start // PACK, cols.stop // PACK)
+            nc.vector.tensor_tensor(
+                product[k][:, block, :, rows].rearrange("p j (b q) -> p b j q", q=RUN),
+                bank[:, cols].rearrange("p (b j q) -> p b j q", j=PACK, q=RUN),
+                left[k][:, block, cols].rearrange("p (b j q) -> p b j q", j=PACK, q=RUN),
+                MULT,
+            )
+
+        left_a = project_left(w1a)
+        w2a_grouped = group(nc.scalar.copy, w2_raw[0], "right_weights")
         w1b_grouped = group(nc.vector.tensor_copy, w1_raw[1], "left_weights")
-        w2b_grouped = group(nc.scalar.copy, w2_raw[1], "right_weights")
-        nc.vector.tensor_tensor(product[0][:, :, :, low], right_a[0], left_a[0][:], MULT)
+        quantise_w2(w2a_grouped, first_half)
         w1b = quantise("w1b", w1b_grouped, HALF)
-        nc.vector.tensor_tensor(left_a[2][:], left_banks[2], left_a[1][:], ADD)
-        left_banks = [project(fields, w1b) for fields in ([0], [0, 1], [2])]
-        w2b = quantise("w2b", w2b_grouped, HALF)
-        left_b = left_tiles(1)
+        for k in range(2):
+            nc.scalar.copy(left[k][:, :, first_half], left_a[k][:])
+        right = [psum.tile([P, H], F32, name="bank", tag="bank") for k in range(3)]
         for k in range(3):
-            nc.scalar.copy(left_b[k][:], left_banks[k])
-        right_b = [project(fields, w2b) for fields in ([1], [2, 3], [3])]
+            project(right[k][:, first_half], [k + 1], 0, w2_code[:, first_half], w2_scale[:, first_half])
+        left_b = project_left(w1b)
+        w2b_grouped = group(nc.scalar.copy, w2_raw[1], "right_weights")
+        multiply(0, 0, right[0], first_half)
+        nc.vector.tensor_tensor(left[2][:, 0, first_half], left_a[2][:, 0, :], left[1][:, 0, first_half], ADD)
+        quantise_w2(w2b_grouped, second_half)
+        for k in range(2):
+            nc.scalar.copy(left[k][:, :, second_half], left_b[k][:])
+        nc.scalar.copy(left[2][:, 1, first_half], left_a[2][:, 1, :])
         for k in (1, 2):
-            nc.vector.tensor_tensor(product[k][:, :, :, low], right_a[k], left_a[k][:], MULT)
-        for block in range(BLOCKS):
-            for k in range(3):
-                nc.vector.tensor_tensor(product[k][:, block, :, high], right_b[k][:, block], left_b[k][:, block], MULT)
+            multiply(k, 0, right[k], first_half)
+        for k in range(3):
+            project(right[k][:, second_half], [k + 1], 0, w2_code[:, second_half], w2_scale[:, second_half])
+        for k in range(2):
+            multiply(k, 0, right[k], second_half)
+        nc.vector.tensor_tensor(left[2][:, 0, second_half], left_b[2][:, 0, :], left[1][:, 0, second_half], ADD)
+        multiply(2, 0, right[2], second_half)
+        nc.scalar.copy(left[2][:, 1, second_half], left_b[2][:, 1, :])
+        for k, fields in enumerate(([1], [2, 3], [3])):
+            bank = psum.tile([P, H], F32, name="bank", tag="bank")
+            project(bank[:], fields, 1, w2_code[:], w2_scale[:])
+            multiply(k, 1, bank, whole)
 
         w3_grouped = keep.tile([P, PACK, P, PACK], BF16, name="w3_grouped", align_bytes=64)
-        for copy, raw, rows in zip((nc.scalar.copy, nc.vector.tensor_copy), w3_raw, (low, high)):
-            copy(
-                w3_grouped[:, :, rows, :].rearrange("p t m j -> p m j t"),
-                raw[:].rearrange("p j (m t) -> p m j t", t=PACK),
-            )
+        w3_dealt = w3_grouped[:].rearrange("p t m j -> p m j t")
+        w3_read = w3_raw[:].rearrange("p j (m t) -> p m j t", t=PACK)
+        for part in range(4):
+            copy = nc.vector.tensor_copy if part == 3 else nc.scalar.copy
+            copy(w3_dealt[:, 32 * part : 32 * (part + 1)], w3_read[:, 32 * part : 32 * (part + 1)])
         w3_code, w3_scale = quantise("w3q", w3_grouped[:].rearrange("p t m j -> p (t m j)"), N)
 
         z_grouped = []

@@ -117,12 +117,12 @@ def tile_picked_zfibi_none_po_kernel(
         def quantise_w2(grouped, cols):
             nc.vector.quantize_mx(out=w2_code[:, cols].bitcast(FP8X4), scales=w2_scale[:, cols], in_=grouped)
 
-        def multiply(k, block, bank, cols):
+        def multiply(k, block, bank, cols, slots=slice(0, PACK)):
             rows = slice(cols.start // PACK, cols.stop // PACK)
             nc.vector.tensor_tensor(
-                product[k][:, block, :, rows].rearrange("p j (b q) -> p b j q", q=RUN),
-                bank[:, cols].rearrange("p (b j q) -> p b j q", j=PACK, q=RUN),
-                left[k][:, block, cols].rearrange("p (b j q) -> p b j q", j=PACK, q=RUN),
+                product[k][:, block, slots, rows].rearrange("p j (b q) -> p b j q", q=RUN),
+                bank[:, cols].rearrange("p (b j q) -> p b j q", j=PACK, q=RUN)[:, :, slots],
+                left[k][:, block, cols].rearrange("p (b j q) -> p b j q", j=PACK, q=RUN)[:, :, slots],
                 MULT,
             )
 
@@ -141,29 +141,28 @@ def tile_picked_zfibi_none_po_kernel(
         multiply(0, 0, right[0], first_half)
         nc.vector.tensor_tensor(left[2][:, 0, first_half], left_a[2][:, 0, :], left[1][:, 0, first_half], ADD)
         quantise_w2(w2b_grouped, second_half)
-        for k in range(2):
+        for k in range(3):
             nc.scalar.copy(left[k][:, :, second_half], left_b[k][:])
         nc.scalar.copy(left[2][:, 1, first_half], left_a[2][:, 1, :])
         for k in (1, 2):
             multiply(k, 0, right[k], first_half)
-        for k in range(3):
-            project(right[k][:, second_half], [k + 1], 0, w2_code[:, second_half], w2_scale[:, second_half])
-        for k in range(2):
+        for k, fields in enumerate(([1], [2, 3], [3])):
+            project(right[k][:, second_half], fields, 0, w2_code[:, second_half], w2_scale[:, second_half])
             multiply(k, 0, right[k], second_half)
-        nc.vector.tensor_tensor(left[2][:, 0, second_half], left_b[2][:, 0, :], left[1][:, 0, second_half], ADD)
-        multiply(2, 0, right[2], second_half)
-        nc.scalar.copy(left[2][:, 1, second_half], left_b[2][:, 1, :])
         for k, fields in enumerate(([1], [2, 3], [3])):
             bank = psum.tile([P, H], F32, name="bank", tag="bank")
             project(bank[:], fields, 1, w2_code[:], w2_scale[:])
-            multiply(k, 1, bank, whole)
+            for slots in ((slice(0, 2), slice(2, 4)) if k == 2 else (slice(0, 4),)):
+                multiply(k, 1, bank, whole, slots)
 
-        w3_grouped = keep.tile([P, PACK, P, PACK], BF16, name="w3_grouped", align_bytes=64)
-        w3_dealt = w3_grouped[:].rearrange("p t m j -> p m j t")
-        w3_read = w3_raw[:].rearrange("p j (m t) -> p m j t", t=PACK)
-        for part in range(4):
-            copy = nc.vector.tensor_copy if part == 3 else nc.scalar.copy
-            copy(w3_dealt[:, 32 * part : 32 * (part + 1)], w3_read[:, 32 * part : 32 * (part + 1)])
+        w3_grouped = keep.tile([P, PACK, P, PACK], BF16, name="w3_grouped", tag="right_weights", align_bytes=64)
+        w3_read = w3_raw[:].rearrange("p j (m t) -> p t m j", t=PACK)
+        nc.gpsimd.tensor_scalar(w3_grouped[:, :, low, :], w3_read[:, :, low, :], 1.0, 0.0, MULT, ADD)
+        for rows in (slice(64, 96), slice(96, 128)):
+            nc.scalar.copy(
+                w3_grouped[:, :, rows, :].rearrange("p t m j -> p m j t"),
+                w3_read[:, :, rows, :].rearrange("p t m j -> p m j t"),
+            )
         w3_code, w3_scale = quantise("w3q", w3_grouped[:].rearrange("p t m j -> p (t m j)"), N)
 
         z_grouped = []

@@ -22,7 +22,6 @@ QUADRANT = 32
 HALF = H // 2
 BLOCKS = V // P
 LINE = 4
-RUN = 8
 
 
 def tile_picked_zfibi_none_po_kernel(
@@ -31,29 +30,25 @@ def tile_picked_zfibi_none_po_kernel(
     nc = tc.nc
     with ExitStack() as ctx:
         keep = ctx.enter_context(tc.tile_pool(name="keep", bufs=1))
+        shared = ctx.enter_context(tc.tile_pool(name="shared", bufs=1))
         psum = ctx.enter_context(tc.psum_pool(name="psum", bufs=8))
 
-        def load(name, weight, half):
-            raw = keep.tile([P, PACK, HALF], F32, name=name, align_bytes=64)
+        def load(tag, weight, half):
+            raw = keep.tile([P, PACK, HALF], F32, name="raw", tag=tag, align_bytes=64)
             rows = weight.rearrange("(p j) c -> p j c", j=PACK)
             nc.sync.dma_start(raw[:], rows[:, :, half * HALF : (half + 1) * HALF])
             return raw
 
         offsets = keep.tile([P, S // 16], U16, name="offsets")
-        scale_table = keep.tile([P, T], U8, name="scale_table", align_bytes=64)
+        scale_table = keep.tile([P, T], U8, name="scale_table", tag="w2_raw0", align_bytes=64)
         nc.vector.memset(scale_table[:].bitcast(I32), 0)
-        w1_raw = [load("w1_raw0", w1, 0)]
+        x_scale = keep.tile([P, S], U8, name="x_scale", align_bytes=64)
+        nc.vector.memset(x_scale[:].bitcast(I32), 0)
+        w1_raw = [load("w1_raw", w1, 0)]
         nc.sync.dma_start(offsets[:], offs)
-        for r in range(4):
-            nc.sync.dma_start(scale_table[r:P:QUADRANT, :].bitcast(I32), x_scales[0, r:16:4, :].bitcast(I32))
+        nc.sync.dma_start(scale_table[0:P:8, :].bitcast(I32), x_scales[0].bitcast(I32))
         word_table = keep.tile([P, T], U32, name="word_table", align_bytes=64)
         nc.sync.dma_start(word_table[:].bitcast(I32), x_words[0].rearrange("p n t -> p (n t)").bitcast(I32))
-        w2_raw = [load("w2_raw0", w2, 0)]
-        w1_raw.append(load("w1_raw1", w1, 1))
-        w2_raw.append(load("w2_raw1", w2, 1))
-        w3_raw = keep.tile([P, PACK, N], F32, name="w3_raw", align_bytes=64)
-        for j in range(PACK):
-            nc.sync.dma_start(w3_raw[:, j, :], w3.rearrange("(b j q) c -> j b q c", j=PACK, q=RUN)[j])
 
         identity = keep.tile([P, P], F32, name="identity", align_bytes=64)
         make_identity(nc, identity[:])
@@ -64,9 +59,10 @@ def tile_picked_zfibi_none_po_kernel(
                 planes.rearrange("p j (c i) -> p c j i", i=LINE),
             )
 
-        def group(copy, raw, tag):
-            grouped = keep.tile([P, HALF, PACK], BF16, name="grouped", tag=tag, align_bytes=64)
-            interleave(copy, grouped[:], raw[:])
+        def stage(tag):
+            return keep.tile([P, HALF, PACK], BF16, name="grouped", tag=tag, align_bytes=64)
+
+        def flat(grouped):
             return grouped[:].rearrange("p c j -> p (c j)")
 
         def quantise(name, grouped, width):
@@ -75,95 +71,120 @@ def tile_picked_zfibi_none_po_kernel(
             nc.vector.quantize_mx(out=codes[:].bitcast(FP8X4), scales=scales[:], in_=grouped)
             return codes, scales
 
-        w1a = quantise("w1a", group(nc.scalar.copy, w1_raw[0], "left_weights"), HALF)
+        w1a_grouped = stage("w2_raw1")
+        interleave(nc.scalar.copy, w1a_grouped[:], w1_raw[0][:])
+        w1a = quantise("w1a", flat(w1a_grouped), HALF)
 
-        x_scale = keep.tile([P, S], U8, name="x_scale", align_bytes=64)
-        nc.vector.tensor_copy(x_scale[:], scale_table[:].indirect(offsets[:]))
+        x_spread = keep.tile([P, S], U8, name="x_spread", tag="w3_raw", align_bytes=64)
+        nc.vector.tensor_copy(x_spread[:], scale_table[:].indirect(offsets[:]))
+        for r in range(4):
+            queue = nc.scalar if r % 2 else nc.sync
+            queue.dma_start(x_scale[r:P:QUADRANT, :].bitcast(I32), x_spread[8 * r : P : QUADRANT, :].bitcast(I32))
+        w2_raw = [load("w2_raw0", w2, 0)]
+        w1_raw.append(load("w1_raw", w1, 1))
+        w2_raw.append(load("w2_raw1", w2, 1))
+        w3_raw = keep.tile([P, PACK, N], F32, name="w3_raw", align_bytes=64)
+        nc.sync.dma_start(w3_raw[:], w3.rearrange("(p j) c -> p j c", j=PACK))
         x_code = []
         for pair in range(2):
             gathered = keep.tile([P, 2 * V], U32, name=f"x_code{pair}", align_bytes=64)
             nc.vector.tensor_copy(gathered[:], word_table[:].indirect(offsets[:, 32 * pair : 32 * (pair + 1)]))
             x_code.append(gathered)
 
-        def project(out, fields, block, codes, scales):
+        def project(out, fields, block, weight):
             for n, d in enumerate(fields):
                 first = d * V + block * P
                 nc.tensor.matmul_mx(
                     out=out,
                     lhsT=x_code[d // 2][:, first % (2 * V) : first % (2 * V) + P].bitcast(FP8X4),
                     lhsT_scale=x_scale[:, first : first + P],
-                    rhs=codes.bitcast(FP8X4),
-                    rhs_scale=scales,
+                    rhs=weight[0][:].bitcast(FP8X4),
+                    rhs_scale=weight[1][:],
                     start=(n == 0),
                     stop=(n == len(fields) - 1),
                 )
 
-        def project_left(weight):
+        def project_pairs(pairs, weight):
             banks = []
-            for fields in ([0], [0, 1], [2]):
-                bank = psum.tile([P, BLOCKS, HALF], F32, name="bank", tag="bank")
-                for block in range(BLOCKS):
-                    project(bank[:, block, :], fields, block, weight[0][:], weight[1][:])
+            for pair in pairs:
+                bank = psum.tile([P, 2, HALF], F32, name="bank", tag="bank")
+                for place, (block, fields) in enumerate(pair):
+                    project(bank[:, place, :], fields, block, weight)
                 banks.append(bank)
             return banks
 
-        left = [keep.tile([P, BLOCKS, H], F32, name=f"left{k}", align_bytes=64) for k in range(3)]
-        product = [keep.tile([P, BLOCKS, PACK, P], F32, name=f"product{k}", align_bytes=64) for k in range(3)]
-        w2_code = keep.tile([P, H], U32, name="w2_code", align_bytes=64)
-        w2_scale = keep.tile([P, H], U8, name="w2_scale", align_bytes=64)
-        first_half, second_half, whole = slice(0, HALF), slice(HALF, H), slice(0, H)
+        def dealt(columns):
+            return columns.rearrange("p (m j) -> p j m", j=PACK)
+
+        def evict(tag, bank, places=slice(0, 2)):
+            left = keep.tile([P, 2, PACK, P // 2], F32, name="left", tag=tag, align_bytes=64)
+            nc.scalar.copy(left[:, places], bank[:, places, :].rearrange("p s (m j) -> p s j m", j=PACK))
+            return left
+
+        product = [keep.tile([P, BLOCKS, PACK, P], F32, name="product0", align_bytes=64)]
         low, high = slice(0, P // 2), slice(P // 2, P)
 
-        def quantise_w2(grouped, cols):
-            nc.vector.quantize_mx(out=w2_code[:, cols].bitcast(FP8X4), scales=w2_scale[:, cols], in_=grouped)
-
-        def multiply(k, block, bank, cols, slots=slice(0, PACK)):
-            rows = slice(cols.start // PACK, cols.stop // PACK)
+        def multiply(k, blocks, rows, right, left, slots=slice(0, PACK)):
             nc.vector.tensor_tensor(
-                product[k][:, block, slots, rows].rearrange("p j (b q) -> p b j q", q=RUN),
-                bank[:, cols].rearrange("p (b j q) -> p b j q", j=PACK, q=RUN)[:, :, slots],
-                left[k][:, block, cols].rearrange("p (b j q) -> p b j q", j=PACK, q=RUN)[:, :, slots],
+                product[k][:, blocks, slots, rows],
+                right.rearrange("p s (m j) -> p s j m", j=PACK)[:, :, slots],
+                left[:, :, slots],
                 MULT,
             )
 
-        left_a = project_left(w1a)
-        w2a_grouped = group(nc.scalar.copy, w2_raw[0], "right_weights")
-        w1b_grouped = group(nc.vector.tensor_copy, w1_raw[1], "left_weights")
-        quantise_w2(w2a_grouped, first_half)
-        w1b = quantise("w1b", w1b_grouped, HALF)
-        for k in range(2):
-            nc.scalar.copy(left[k][:, :, first_half], left_a[k][:])
-        right = [psum.tile([P, H], F32, name="bank", tag="bank") for k in range(3)]
-        for k in range(3):
-            project(right[k][:, first_half], [k + 1], 0, w2_code[:, first_half], w2_scale[:, first_half])
-        left_b = project_left(w1b)
-        w2b_grouped = group(nc.scalar.copy, w2_raw[1], "right_weights")
-        multiply(0, 0, right[0], first_half)
-        nc.vector.tensor_tensor(left[2][:, 0, first_half], left_a[2][:, 0, :], left[1][:, 0, first_half], ADD)
-        quantise_w2(w2b_grouped, second_half)
-        for k in range(3):
-            nc.scalar.copy(left[k][:, :, second_half], left_b[k][:])
-        nc.scalar.copy(left[2][:, 1, first_half], left_a[2][:, 1, :])
-        for k in (1, 2):
-            multiply(k, 0, right[k], first_half)
-        for k, fields in enumerate(([1], [2, 3], [3])):
-            project(right[k][:, second_half], fields, 0, w2_code[:, second_half], w2_scale[:, second_half])
-            multiply(k, 0, right[k], second_half)
-        for k, fields in enumerate(([1], [2, 3], [3])):
-            bank = psum.tile([P, H], F32, name="bank", tag="bank")
-            project(bank[:], fields, 1, w2_code[:], w2_scale[:])
-            for slots in ((slice(0, 2), slice(2, 4)) if k == 2 else (slice(0, 4),)):
-                multiply(k, 1, bank, whole, slots)
+        left_fields = ([0], [0, 1], [2])
+        right_fields = ([1], [2, 3], [3])
+        by_term = [[(0, k), (1, k)] for k in range(3)]
+        by_block = [[(0, 0), (0, 1)], [(0, 2), (1, 0)], [(1, 1), (1, 2)]]
 
-        w3_grouped = keep.tile([P, PACK, P, PACK], BF16, name="w3_grouped", tag="right_weights", align_bytes=64)
+        first_left = [[(0, [0]), (1, [0])], [(1, [0, 1]), (0, [2])], [(1, [2]), (0, [1])]]
+        left_a_banks = project_pairs(first_left, w1a)
+        w2a_grouped = stage("w2a")
+        interleave(nc.scalar.copy, w2a_grouped[:], w2_raw[0][:])
+        w2a = quantise("w2a", flat(w2a_grouped), HALF)
+        w1b_grouped = shared.tile([P, HALF, PACK], BF16, name="w1b_grouped", offset=1024, align_bytes=64)
+        interleave(nc.vector.tensor_copy, w1b_grouped[:], w1_raw[1][:])
+        left_a = keep.tile([P, 3 * BLOCKS, PACK, P // 2], F32, name="left_a", tag="w2_raw0", align_bytes=64)
+        for bank, places, slots in zip(left_a_banks, (slice(0, 2), slice(0, 2), slice(0, 1)), (slice(0, 2), slice(3, 5), slice(5, 6))):
+            nc.scalar.copy(left_a[:, slots], bank[:, places, :].rearrange("p s (m j) -> p s j m", j=PACK))
+        nc.vector.tensor_tensor(left_a[:, 2], dealt(left_a_banks[2][:, 1, :]), left_a[:, 0], ADD)
+        w1b = quantise("w1b", flat(w1b_grouped), HALF)
+        right_a = project_pairs([[(b, right_fields[k]) for b, k in pair] for pair in by_term], w2a)
+        left_b_banks = project_pairs([[(b, left_fields[k]) for b, k in pair] for pair in by_block], w1b)
+
+        w2b_grouped = shared.tile([P, HALF, PACK], BF16, name="w2b_grouped", offset=1024, align_bytes=64)
+        interleave(nc.scalar.copy, w2b_grouped[:, :P, :], w2_raw[1][:, :, :P])
+        nc.gpsimd.tensor_scalar(
+            w2b_grouped[:, P:, :], w2_raw[1][:, :, P:].rearrange("p j c -> p c j"), 1.0, 0.0, MULT, ADD
+        )
+        w2b = quantise("w2b", flat(w2b_grouped), HALF)
+        product.append(keep.tile([P, BLOCKS, PACK, P], F32, name="product1", align_bytes=64))
+        product.append(shared.tile([P, BLOCKS, PACK, P], F32, name="product2", offset=2048, align_bytes=64))
+        for k in range(3):
+            multiply(k, slice(0, BLOCKS), low, right_a[k][:], left_a[:, 2 * k : 2 * k + 2])
+
+        left_b = [evict(tag, bank) for tag, bank in zip(("w2_raw1", "left_b1", "left_b2"), left_b_banks)]
+        right_b = project_pairs([[(b, right_fields[k]) for b, k in pair] for pair in by_block], w2b)
+        for n, pair in enumerate(by_block):
+            for place, (block, k) in enumerate(pair):
+                here = slice(place, place + 1)
+                for slots in ((slice(0, 2), slice(2, 4)) if (block, k) == (1, 2) else (slice(0, 4),)):
+                    multiply(k, slice(block, block + 1), high, right_b[n][:, here, :], left_b[n][:, here], slots)
+
+        w3_code = keep.tile([P, N], U32, name="w3_code", align_bytes=64)
+        w3_scale = keep.tile([P, N], U8, name="w3_scale", align_bytes=64)
         w3_read = w3_raw[:].rearrange("p j (m t) -> p t m j", t=PACK)
-        nc.gpsimd.tensor_scalar(w3_grouped[:, :, low, :], w3_read[:, :, low, :], 1.0, 0.0, MULT, ADD)
-        for rows in (slice(64, 96), slice(96, 128)):
-            nc.scalar.copy(
-                w3_grouped[:, :, rows, :].rearrange("p t m j -> p m j t"),
-                w3_read[:, :, rows, :].rearrange("p t m j -> p m j t"),
+        w3_front = shared.tile([P, 2, P, PACK], BF16, name="w3_front", offset=0, align_bytes=64)
+        nc.gpsimd.tensor_scalar(w3_front[:], w3_read[:, :2], 1.0, 0.0, MULT, ADD)
+        w3_back = keep.tile([P, 2, P, PACK], BF16, name="w3_back", tag="w2_raw1", align_bytes=64)
+        nc.scalar.copy(w3_back[:].rearrange("p t m j -> p m j t"), w3_read[:, 2:].rearrange("p t m j -> p m j t"))
+        for half, grouped in enumerate((w3_front, w3_back)):
+            cols = slice(half * HALF, (half + 1) * HALF)
+            nc.vector.quantize_mx(
+                out=w3_code[:, cols].bitcast(FP8X4),
+                scales=w3_scale[:, cols],
+                in_=grouped[:].rearrange("p t m j -> p (t m j)"),
             )
-        w3_code, w3_scale = quantise("w3q", w3_grouped[:].rearrange("p t m j -> p (t m j)"), N)
 
         z_grouped = []
         for block in range(BLOCKS):

@@ -22,6 +22,7 @@ QUADRANT = 32
 HALF = H // 2
 BLOCKS = V // P
 LINE = 4
+HEAD = 3 * T // 16
 
 
 def tile_picked_zfibi_none_po_kernel(
@@ -44,11 +45,13 @@ def tile_picked_zfibi_none_po_kernel(
         nc.vector.memset(scale_table[:].bitcast(I32), 0)
         x_scale = keep.tile([P, S], U8, name="x_scale", align_bytes=64)
         nc.vector.memset(x_scale[:].bitcast(I32), 0)
-        w1_raw = [load("w1_raw", w1, 0)]
-        nc.sync.dma_start(offsets[:], offs)
-        nc.sync.dma_start(scale_table[0:P:8, :].bitcast(I32), x_scales[0].bitcast(I32))
         word_table = keep.tile([P, T], U32, name="word_table", align_bytes=64)
-        nc.sync.dma_start(word_table[:].bitcast(I32), x_words[0].rearrange("p n t -> p (n t)").bitcast(I32))
+        words = x_words[0].rearrange("p n t -> p (n t)").bitcast(I32)
+        nc.sync.dma_start(word_table[:, :HEAD].bitcast(I32), words[:, :HEAD])
+        nc.sync.dma_start(scale_table[0:P:8, :].bitcast(I32), x_scales[0].bitcast(I32))
+        nc.sync.dma_start(offsets[:], offs)
+        w1_raw = [load("w1_raw", w1, 0)]
+        nc.sync.dma_start(word_table[:, HEAD:].bitcast(I32), words[:, HEAD:])
 
         identity = keep.tile([P, P], F32, name="identity", align_bytes=64)
         make_identity(nc, identity[:])

@@ -32,16 +32,20 @@ def tile_picked_zfibi_none_po_kernel(
     with ExitStack() as ctx:
         keep = ctx.enter_context(tc.tile_pool(name="keep", bufs=1))
         shared = ctx.enter_context(tc.tile_pool(name="shared", bufs=1))
+        early = ctx.enter_context(tc.tile_pool(name="early", bufs=1))
         psum = ctx.enter_context(tc.psum_pool(name="psum", bufs=8))
 
-        def load(tag, weight, half):
-            raw = keep.tile([P, PACK, HALF], F32, name="raw", tag=tag, align_bytes=64)
+        def load(raw, weight, half):
             rows = weight.rearrange("(p j) c -> p j c", j=PACK)
             nc.sync.dma_start(raw[:], rows[:, :, half * HALF : (half + 1) * HALF])
             return raw
 
+        warm_up = keep.tile([P, 16], F32, name="warm_up")
+        nc.gpsimd.memset(warm_up[:, :8], 0.0)
+        nc.scalar.copy(warm_up[:, 8:], warm_up[:, :8])
+
         offsets = keep.tile([P, S // 16], U16, name="offsets")
-        scale_table = keep.tile([P, T], U8, name="scale_table", tag="w2_raw0", align_bytes=64)
+        scale_table = early.tile([P, T], U8, name="scale_table", offset=2048, align_bytes=64)
         nc.vector.memset(scale_table[:].bitcast(I32), 0)
         x_scale = keep.tile([P, S], U8, name="x_scale", align_bytes=64)
         nc.vector.memset(x_scale[:].bitcast(I32), 0)
@@ -50,7 +54,7 @@ def tile_picked_zfibi_none_po_kernel(
         nc.sync.dma_start(word_table[:, :HEAD].bitcast(I32), words[:, :HEAD])
         nc.sync.dma_start(scale_table[0:P:8, :].bitcast(I32), x_scales[0].bitcast(I32))
         nc.sync.dma_start(offsets[:], offs)
-        w1_raw = [load("w1_raw", w1, 0)]
+        w1_raw = [load(keep.tile([P, PACK, HALF], F32, name="w1_raw0", tag="w2_raw1", align_bytes=64), w1, 0)]
         nc.sync.dma_start(word_table[:, HEAD:].bitcast(I32), words[:, HEAD:])
 
         identity = keep.tile([P, P], F32, name="identity", align_bytes=64)
@@ -74,7 +78,7 @@ def tile_picked_zfibi_none_po_kernel(
             nc.vector.quantize_mx(out=codes[:].bitcast(FP8X4), scales=scales[:], in_=grouped)
             return codes, scales
 
-        w1a_grouped = stage("w2_raw1")
+        w1a_grouped = stage("w1a")
         interleave(nc.scalar.copy, w1a_grouped[:], w1_raw[0][:])
         w1a = quantise("w1a", flat(w1a_grouped), HALF)
 
@@ -83,9 +87,9 @@ def tile_picked_zfibi_none_po_kernel(
         for r in range(4):
             queue = nc.scalar if r % 2 else nc.sync
             queue.dma_start(x_scale[r:P:QUADRANT, :].bitcast(I32), x_spread[8 * r : P : QUADRANT, :].bitcast(I32))
-        w2_raw = [load("w2_raw0", w2, 0)]
-        w1_raw.append(load("w1_raw", w1, 1))
-        w2_raw.append(load("w2_raw1", w2, 1))
+        w2_raw = [load(early.tile([P, PACK, HALF], F32, name="w2_raw0", offset=4096, align_bytes=64), w2, 0)]
+        w1_raw.append(load(early.tile([P, PACK, HALF], F32, name="w1_raw1", offset=0, align_bytes=64), w1, 1))
+        w2_raw.append(load(keep.tile([P, PACK, HALF], F32, name="w2_raw1", align_bytes=64), w2, 1))
         w3_raw = keep.tile([P, PACK, N], F32, name="w3_raw", align_bytes=64)
         nc.sync.dma_start(w3_raw[:], w3.rearrange("(p j) c -> p j c", j=PACK))
         x_code = []
@@ -147,7 +151,7 @@ def tile_picked_zfibi_none_po_kernel(
         w2a = quantise("w2a", flat(w2a_grouped), HALF)
         w1b_grouped = shared.tile([P, HALF, PACK], BF16, name="w1b_grouped", offset=1024, align_bytes=64)
         interleave(nc.vector.tensor_copy, w1b_grouped[:], w1_raw[1][:])
-        left_a = keep.tile([P, 3 * BLOCKS, PACK, P // 2], F32, name="left_a", tag="w2_raw0", align_bytes=64)
+        left_a = early.tile([P, 3 * BLOCKS, PACK, P // 2], F32, name="left_a", offset=4096, align_bytes=64)
         for bank, places, slots in zip(left_a_banks, (slice(0, 2), slice(0, 2), slice(0, 1)), (slice(0, 2), slice(3, 5), slice(5, 6))):
             nc.scalar.copy(left_a[:, slots], bank[:, places, :].rearrange("p s (m j) -> p s j m", j=PACK))
         nc.vector.tensor_tensor(left_a[:, 2], dealt(left_a_banks[2][:, 1, :]), left_a[:, 0], ADD)

@@ -49,6 +49,9 @@ def tile_picked_zfibi_none_po_kernel(
         nc.vector.memset(scale_table[:].bitcast(I32), 0)
         x_scale = keep.tile([P, S], U8, name="x_scale", align_bytes=64)
         nc.vector.memset(x_scale[:].bitcast(I32), 0)
+        identity = keep.tile([P, P], F32, name="identity", align_bytes=64)
+        nc.vector.memset(identity[:], 0.0)
+        make_identity(nc, identity[:], nomemset=True)
         word_table = keep.tile([P, T], U32, name="word_table", align_bytes=64)
         words = x_words[0].rearrange("p n t -> p (n t)").bitcast(I32)
         nc.sync.dma_start(word_table[:, :HEAD].bitcast(I32), words[:, :HEAD])
@@ -56,9 +59,6 @@ def tile_picked_zfibi_none_po_kernel(
         nc.sync.dma_start(offsets[:], offs)
         w1_raw = [load(keep.tile([P, PACK, HALF], F32, name="w1_raw0", tag="w2_raw1", align_bytes=64), w1, 0)]
         nc.sync.dma_start(word_table[:, HEAD:].bitcast(I32), words[:, HEAD:])
-
-        identity = keep.tile([P, P], F32, name="identity", align_bytes=64)
-        make_identity(nc, identity[:])
 
         def interleave(copy, grouped, planes):
             copy(
@@ -230,20 +230,30 @@ def tile_picked_zfibi_none_po_kernel(
         out_scale = keep.tile([P, V], U8, name="out_scale", align_bytes=64)
         out_words = out_1[0].rearrange("p n t -> p (n t)").bitcast(I32)
         out_rows = out_0.rearrange("(p t) v -> p t v", t=PACK)
-        for block in range(BLOCKS):
-            cols = slice(block * P, (block + 1) * P)
-            result = keep.tile([P, PACK, P], F32, name=f"result{block}", align_bytes=64)
-            out_grouped = keep.tile([P, P, PACK], BF16, name=f"out_grouped{block}", align_bytes=64)
-            for part in (low, high):
-                nc.scalar.copy(result[:, :, part], out_banks[block][:, :, part])
-                interleave(nc.vector.tensor_copy, out_grouped[:, part, :], result[:, :, part])
-            nc.sync.dma_start(out_rows[:, :, cols], result[:])
+
+        def quantise_out(grouped, first, width):
             nc.vector.quantize_mx(
-                out=out_code[:, cols].bitcast(FP8X4),
-                scales=out_scale[:, cols],
-                in_=out_grouped[:].rearrange("p v t -> p (v t)"),
+                out=out_code[:, first : first + width].bitcast(FP8X4),
+                scales=out_scale[:, first : first + width],
+                in_=grouped.rearrange("p v t -> p (v t)"),
             )
-            nc.sync.dma_start(out_words[:, cols], out_code[:, cols].bitcast(I32))
+
+        result = [keep.tile([P, PACK, P], F32, name=f"result{block}", align_bytes=64) for block in range(BLOCKS)]
+        out_grouped = [keep.tile([P, P, PACK], BF16, name=f"out_grouped{block}", align_bytes=64) for block in range(BLOCKS)]
+        for part in (low, high):
+            nc.scalar.copy(result[0][:, :, part], out_banks[0][:, :, part])
+            interleave(nc.vector.tensor_copy, out_grouped[0][:, part, :], result[0][:, :, part])
+        nc.sync.dma_start(out_rows[:, :, :P], result[0][:])
+        quantise_out(out_grouped[0][:], 0, P)
+        nc.sync.dma_start(out_words[:, :P], out_code[:, :P].bitcast(I32))
+        nc.scalar.copy(result[1][:, :, low], out_banks[1][:, :, low])
+        interleave(nc.vector.tensor_copy, out_grouped[1][:, low, :], result[1][:, :, low])
+        quantise_out(out_grouped[1][:, low, :], P, P // 2)
+        nc.scalar.copy(result[1][:, :, high], out_banks[1][:, :, high])
+        nc.sync.dma_start(out_rows[:, :, P:], result[1][:])
+        nc.scalar.copy(out_grouped[1][:, high, :], out_banks[1][:, :, high].rearrange("p t v -> p v t"))
+        quantise_out(out_grouped[1][:, high, :], P + P // 2, P // 2)
+        nc.sync.dma_start(out_words[:, P:], out_code[:, P:].bitcast(I32))
 
         for r in range(4):
             queue = nc.scalar if r % 2 else nc.sync

@@ -49,9 +49,6 @@ def tile_picked_zfibi_none_po_kernel(
         nc.vector.memset(scale_table[:].bitcast(I32), 0)
         x_scale = keep.tile([P, S], U8, name="x_scale", align_bytes=64)
         nc.vector.memset(x_scale[:].bitcast(I32), 0)
-        identity = keep.tile([P, P], F32, name="identity", align_bytes=64)
-        nc.vector.memset(identity[:], 0.0)
-        make_identity(nc, identity[:], nomemset=True)
         word_table = keep.tile([P, T], U32, name="word_table", align_bytes=64)
         words = x_words[0].rearrange("p n t -> p (n t)").bitcast(I32)
         nc.sync.dma_start(word_table[:, :HEAD].bitcast(I32), words[:, :HEAD])
@@ -59,6 +56,9 @@ def tile_picked_zfibi_none_po_kernel(
         nc.sync.dma_start(offsets[:], offs)
         w1_raw = [load(keep.tile([P, PACK, HALF], F32, name="w1_raw0", tag="w2_raw1", align_bytes=64), w1, 0)]
         nc.sync.dma_start(word_table[:, HEAD:].bitcast(I32), words[:, HEAD:])
+
+        identity = keep.tile([P, P], F32, name="identity", align_bytes=64)
+        make_identity(nc, identity[:])
 
         def interleave(copy, grouped, planes):
             copy(

@@ -213,18 +213,20 @@ def tile_picked_zfibi_none_po_kernel(
         out_banks = []
         for block in range(BLOCKS):
             z_code, z_scale = quantise(f"zq{block}", z_grouped[block][:].rearrange("p v t -> p (v t)"), P)
-            out_bank = psum.tile([P, PACK, P], F32, name="bank", tag="bank")
-            for t in range(PACK):
-                nc.tensor.matmul_mx(
-                    out=out_bank[:, t, :],
-                    lhsT=w3_code[:, t * P : (t + 1) * P].bitcast(FP8X4),
-                    lhsT_scale=w3_scale[:, t * P : (t + 1) * P],
-                    rhs=z_code[:].bitcast(FP8X4),
-                    rhs_scale=z_scale[:],
-                    start=True,
-                    stop=True,
-                )
-            out_banks.append(out_bank)
+            for pair in range(2):
+                out_bank = psum.tile([P, 2, P], F32, name="bank", tag="bank")
+                for place in range(2):
+                    t = 2 * pair + place
+                    nc.tensor.matmul_mx(
+                        out=out_bank[:, place, :],
+                        lhsT=w3_code[:, t * P : (t + 1) * P].bitcast(FP8X4),
+                        lhsT_scale=w3_scale[:, t * P : (t + 1) * P],
+                        rhs=z_code[:].bitcast(FP8X4),
+                        rhs_scale=z_scale[:],
+                        start=True,
+                        stop=True,
+                    )
+                out_banks.append(out_bank)
 
         out_code = keep.tile([P, V], U32, name="out_code", align_bytes=64)
         out_scale = keep.tile([P, V], U8, name="out_scale", align_bytes=64)
@@ -238,22 +240,24 @@ def tile_picked_zfibi_none_po_kernel(
                 in_=grouped.rearrange("p v t -> p (v t)"),
             )
 
-        result = [keep.tile([P, PACK, P], F32, name=f"result{block}", align_bytes=64) for block in range(BLOCKS)]
-        out_grouped = [keep.tile([P, P, PACK], BF16, name=f"out_grouped{block}", align_bytes=64) for block in range(BLOCKS)]
-        for part in (low, high):
-            nc.scalar.copy(result[0][:, :, part], out_banks[0][:, :, part])
-            interleave(nc.vector.tensor_copy, out_grouped[0][:, part, :], result[0][:, :, part])
-        nc.sync.dma_start(out_rows[:, :, :P], result[0][:])
-        quantise_out(out_grouped[0][:], 0, P)
-        nc.sync.dma_start(out_words[:, :P], out_code[:, :P].bitcast(I32))
-        nc.scalar.copy(result[1][:, :, low], out_banks[1][:, :, low])
-        interleave(nc.vector.tensor_copy, out_grouped[1][:, low, :], result[1][:, :, low])
-        quantise_out(out_grouped[1][:, low, :], P, P // 2)
-        nc.scalar.copy(result[1][:, :, high], out_banks[1][:, :, high])
-        nc.sync.dma_start(out_rows[:, :, P:], result[1][:])
-        nc.scalar.copy(out_grouped[1][:, high, :], out_banks[1][:, :, high].rearrange("p t v -> p v t"))
-        quantise_out(out_grouped[1][:, high, :], P + P // 2, P // 2)
-        nc.sync.dma_start(out_words[:, P:], out_code[:, P:].bitcast(I32))
+        for block in range(BLOCKS):
+            cols = slice(block * P, (block + 1) * P)
+            result = keep.tile([P, PACK, P], F32, name=f"result{block}", align_bytes=64)
+            out_grouped = keep.tile([P, P, PACK], BF16, name=f"out_grouped{block}", align_bytes=64)
+            for pair in range(2):
+                slots = slice(2 * pair, 2 * pair + 2)
+                nc.scalar.copy(result[:, slots, :], out_banks[2 * block + pair][:])
+                if block == 0:
+                    nc.sync.dma_start(out_rows[:, slots, cols], result[:, slots, :])
+            if block == 0:
+                interleave(nc.vector.tensor_copy, out_grouped[:], result[:])
+                quantise_out(out_grouped[:], 0, P)
+            else:
+                nc.sync.dma_start(out_rows[:, :, cols], result[:])
+                for part, copy in ((low, nc.vector.tensor_copy), (high, nc.scalar.copy)):
+                    interleave(copy, out_grouped[:, part, :], result[:, :, part])
+                    quantise_out(out_grouped[:, part, :], P + part.start, P // 2)
+        nc.sync.dma_start(out_words, out_code[:].bitcast(I32))
 
         for r in range(4):
             queue = nc.scalar if r % 2 else nc.sync

@@ -195,19 +195,20 @@ def tile_picked_zfibi_none_po_kernel(
 
         z_grouped = []
         for block in range(BLOCKS):
-            z_bank = psum.tile([P, PACK, P], F32, name="bank", tag="bank")
-            for k in range(3):
-                for t in range(PACK):
-                    nc.tensor.matmul(
-                        z_bank[:, t, :],
-                        product[k][:, block, t, :],
-                        identity[:],
-                        start=(k == 0 and t == 0),
-                        stop=(k == 2 and t == PACK - 1),
-                        is_transpose=True,
-                    )
             grouped = keep.tile([P, P, PACK], BF16, name=f"z_grouped{block}", align_bytes=64)
-            nc.scalar.copy(grouped[:], z_bank[:].rearrange("p t v -> p v t"))
+            for slots in ([0, 1, 2, 3],) if block == 0 else ([0, 1], [2, 3]):
+                z_bank = psum.tile([P, len(slots), P], F32, name="bank", tag="bank")
+                for k in range(3):
+                    for place, t in enumerate(slots):
+                        nc.tensor.matmul(
+                            z_bank[:, place, :],
+                            product[k][:, block, t, :],
+                            identity[:],
+                            start=(k == 0 and place == 0),
+                            stop=(k == 2 and place == len(slots) - 1),
+                            is_transpose=True,
+                        )
+                nc.scalar.copy(grouped[:, :, slots[0] : slots[-1] + 1], z_bank[:].rearrange("p t v -> p v t"))
             z_grouped.append(grouped)
 
         out_banks = []
@@ -247,13 +248,11 @@ def tile_picked_zfibi_none_po_kernel(
             for pair in range(2):
                 slots = slice(2 * pair, 2 * pair + 2)
                 nc.scalar.copy(result[:, slots, :], out_banks[2 * block + pair][:])
-                if block == 0:
-                    nc.sync.dma_start(out_rows[:, slots, cols], result[:, slots, :])
+                nc.sync.dma_start(out_rows[:, slots, cols], result[:, slots, :])
             if block == 0:
                 interleave(nc.vector.tensor_copy, out_grouped[:], result[:])
                 quantise_out(out_grouped[:], 0, P)
             else:
-                nc.sync.dma_start(out_rows[:, :, cols], result[:])
                 for part, copy in ((low, nc.vector.tensor_copy), (high, nc.scalar.copy)):
                     interleave(copy, out_grouped[:, part, :], result[:, :, part])
                     quantise_out(out_grouped[:, part, :], P + part.start, P // 2)

@@ -22,7 +22,6 @@ QUADRANT = 32
 HALF = H // 2
 BLOCKS = V // P
 LINE = 4
-HEAD = 3 * T // 16
 
 
 def tile_picked_zfibi_none_po_kernel(
@@ -46,16 +45,15 @@ def tile_picked_zfibi_none_po_kernel(
 
         offsets = keep.tile([P, S // 16], U16, name="offsets")
         scale_table = early.tile([P, T], U8, name="scale_table", offset=2048, align_bytes=64)
-        nc.vector.memset(scale_table[:].bitcast(I32), 0)
+        nc.vector.memset(scale_table[: P - 16, :].bitcast(I32), 0)
         x_scale = keep.tile([P, S], U8, name="x_scale", align_bytes=64)
         nc.vector.memset(x_scale[:].bitcast(I32), 0)
         word_table = keep.tile([P, T], U32, name="word_table", align_bytes=64)
         words = x_words[0].rearrange("p n t -> p (n t)").bitcast(I32)
-        nc.sync.dma_start(word_table[:, :HEAD].bitcast(I32), words[:, :HEAD])
-        nc.sync.dma_start(scale_table[0:P:8, :].bitcast(I32), x_scales[0].bitcast(I32))
+        nc.sync.dma_start(scale_table[P - 16 :, :].bitcast(I32), x_scales[0].bitcast(I32))
         nc.sync.dma_start(offsets[:], offs)
         w1_raw = [load(keep.tile([P, PACK, HALF], F32, name="w1_raw0", tag="w2_raw1", align_bytes=64), w1, 0)]
-        nc.sync.dma_start(word_table[:, HEAD:].bitcast(I32), words[:, HEAD:])
+        nc.sync.dma_start(word_table[:].bitcast(I32), words)
 
         identity = keep.tile([P, P], F32, name="identity", align_bytes=64)
         make_identity(nc, identity[:])
@@ -84,9 +82,12 @@ def tile_picked_zfibi_none_po_kernel(
 
         x_spread = keep.tile([P, S], U8, name="x_spread", tag="w3_raw", align_bytes=64)
         nc.vector.tensor_copy(x_spread[:], scale_table[:].indirect(offsets[:]))
-        for r in range(4):
-            queue = nc.scalar if r % 2 else nc.sync
-            queue.dma_start(x_scale[r:P:QUADRANT, :].bitcast(I32), x_spread[8 * r : P : QUADRANT, :].bitcast(I32))
+        for q in range(4):
+            queue = nc.scalar if q % 2 else nc.sync
+            queue.dma_start(
+                x_scale[QUADRANT * q : QUADRANT * q + 4, :].bitcast(I32),
+                x_spread[P - 16 + 4 * q : P - 12 + 4 * q, :].bitcast(I32),
+            )
         w2_raw = [load(early.tile([P, PACK, HALF], F32, name="w2_raw0", offset=4096, align_bytes=64), w2, 0)]
         w1_raw.append(load(early.tile([P, PACK, HALF], F32, name="w1_raw1", offset=0, align_bytes=64), w1, 1))
         w2_raw.append(load(keep.tile([P, PACK, HALF], F32, name="w2_raw1", align_bytes=64), w2, 1))

@@ -34,9 +34,9 @@ def tile_picked_zfibi_none_po_kernel(
         early = ctx.enter_context(tc.tile_pool(name="early", bufs=1))
         psum = ctx.enter_context(tc.psum_pool(name="psum", bufs=8))
 
-        def load(raw, weight, half):
+        def load(raw, weight, part, width=HALF):
             rows = weight.rearrange("(p j) c -> p j c", j=PACK)
-            nc.sync.dma_start(raw[:], rows[:, :, half * HALF : (half + 1) * HALF])
+            nc.sync.dma_start(raw[:], rows[:, :, part * width : (part + 1) * width])
             return raw
 
         warm_up = keep.tile([P, 16], F32, name="warm_up")
@@ -44,7 +44,7 @@ def tile_picked_zfibi_none_po_kernel(
         nc.scalar.copy(warm_up[:, 8:], warm_up[:, :8])
 
         offsets = keep.tile([P, S // 16], U16, name="offsets")
-        scale_table = early.tile([P, T], U8, name="scale_table", offset=2048, align_bytes=64)
+        scale_table = early.tile([P, T], U8, name="scale_table", offset=3072, align_bytes=64)
         nc.vector.memset(scale_table[: P - 16, :].bitcast(I32), 0)
         x_scale = keep.tile([P, S], U8, name="x_scale", align_bytes=64)
         nc.vector.memset(x_scale[:].bitcast(I32), 0)
@@ -52,7 +52,7 @@ def tile_picked_zfibi_none_po_kernel(
         words = x_words[0].rearrange("p n t -> p (n t)").bitcast(I32)
         nc.sync.dma_start(scale_table[P - 16 :, :].bitcast(I32), x_scales[0].bitcast(I32))
         nc.sync.dma_start(offsets[:], offs)
-        w1_raw = [load(keep.tile([P, PACK, HALF], F32, name="w1_raw0", tag="w2_raw1", align_bytes=64), w1, 0)]
+        w1_first = load(keep.tile([P, PACK, P], F32, name="w1_first", tag="w2_raw1", align_bytes=64), w1, 0, P)
         nc.sync.dma_start(word_table[:].bitcast(I32), words)
 
         identity = keep.tile([P, P], F32, name="identity", align_bytes=64)
@@ -76,9 +76,18 @@ def tile_picked_zfibi_none_po_kernel(
             nc.vector.quantize_mx(out=codes[:].bitcast(FP8X4), scales=scales[:], in_=grouped)
             return codes, scales
 
-        w1a_grouped = stage("w1a")
-        interleave(nc.scalar.copy, w1a_grouped[:], w1_raw[0][:])
-        w1a = quantise("w1a", flat(w1a_grouped), HALF)
+        w1a = (
+            keep.tile([P, HALF], U32, name="w1a_code", align_bytes=64),
+            keep.tile([P, HALF], U8, name="w1a_scale", align_bytes=64),
+        )
+
+        def quantise_quarter(raw, part, tag):
+            grouped = keep.tile([P, P, PACK], BF16, name="quarter", tag=tag, align_bytes=64)
+            interleave(nc.scalar.copy, grouped[:], raw[:])
+            cols = slice(part * P, (part + 1) * P)
+            nc.vector.quantize_mx(out=w1a[0][:, cols].bitcast(FP8X4), scales=w1a[1][:, cols], in_=flat(grouped))
+
+        quantise_quarter(w1_first, 0, "w1_quarter0")
 
         x_spread = keep.tile([P, S], U8, name="x_spread", tag="w3_raw", align_bytes=64)
         nc.vector.tensor_copy(x_spread[:], scale_table[:].indirect(offsets[:]))
@@ -88,26 +97,37 @@ def tile_picked_zfibi_none_po_kernel(
                 x_scale[QUADRANT * q : QUADRANT * q + 4, :].bitcast(I32),
                 x_spread[P - 16 + 4 * q : P - 12 + 4 * q, :].bitcast(I32),
             )
-        w2_raw = [load(early.tile([P, PACK, HALF], F32, name="w2_raw0", offset=4096, align_bytes=64), w2, 0)]
-        w1_raw.append(load(early.tile([P, PACK, HALF], F32, name="w1_raw1", offset=0, align_bytes=64), w1, 1))
+        w1_second = load(early.tile([P, PACK, P], F32, name="w1_second", offset=4096, align_bytes=64), w1, 1, P)
+        w2_raw = [load(early.tile([P, PACK, HALF], F32, name="w2_raw0", offset=6144, align_bytes=64), w2, 0)]
+        w1_back = load(early.tile([P, PACK, HALF], F32, name="w1_back", offset=0, align_bytes=64), w1, 1)
         w2_raw.append(load(keep.tile([P, PACK, HALF], F32, name="w2_raw1", align_bytes=64), w2, 1))
         w3_raw = keep.tile([P, PACK, N], F32, name="w3_raw", align_bytes=64)
         nc.sync.dma_start(w3_raw[:], w3.rearrange("(p j) c -> p j c", j=PACK))
-        x_code = []
-        for pair in range(2):
-            gathered = keep.tile([P, 2 * V], U32, name=f"x_code{pair}", align_bytes=64)
-            nc.vector.tensor_copy(gathered[:], word_table[:].indirect(offsets[:, 32 * pair : 32 * (pair + 1)]))
-            x_code.append(gathered)
+        x_code = {}
 
-        def project(out, fields, block, weight):
+        def gather(fields, tag):
+            gathered = keep.tile([P, len(fields), V], U32, name="gathered", tag=tag, align_bytes=64)
+            columns = slice(fields[0] * V // 16, (fields[-1] + 1) * V // 16)
+            nc.vector.tensor_copy(
+                gathered[:].rearrange("p d v -> p (d v)"), word_table[:].indirect(offsets[:, columns])
+            )
+            for n, d in enumerate(fields):
+                x_code[d] = gathered[:, n, :]
+
+        gather([0, 1], "x_code01")
+        gather([2], "x_code2")
+        quantise_quarter(w1_second, 1, "x_code3")
+        gather([3], "x_code3")
+
+        def project(out, fields, block, weight, cols=slice(0, HALF)):
             for n, d in enumerate(fields):
                 first = d * V + block * P
                 nc.tensor.matmul_mx(
-                    out=out,
-                    lhsT=x_code[d // 2][:, first % (2 * V) : first % (2 * V) + P].bitcast(FP8X4),
+                    out=out[:, cols],
+                    lhsT=x_code[d][:, block * P : (block + 1) * P].bitcast(FP8X4),
                     lhsT_scale=x_scale[:, first : first + P],
-                    rhs=weight[0][:].bitcast(FP8X4),
-                    rhs_scale=weight[1][:],
+                    rhs=weight[0][:, cols].bitcast(FP8X4),
+                    rhs_scale=weight[1][:, cols],
                     start=(n == 0),
                     stop=(n == len(fields) - 1),
                 )
@@ -146,13 +166,21 @@ def tile_picked_zfibi_none_po_kernel(
         by_block = [[(0, 0), (0, 1)], [(0, 2), (1, 0)], [(1, 1), (1, 2)]]
 
         first_left = [[(0, [0]), (1, [0])], [(1, [0, 1]), (0, [2])], [(1, [2]), (0, [1])]]
-        left_a_banks = project_pairs(first_left, w1a)
+        left_a_banks = [psum.tile([P, 2, HALF], F32, name="bank", tag="bank") for pair in first_left]
+        places = [(bank[:, n, :], *pair[n]) for bank, pair in zip(left_a_banks, first_left) for n in range(2)]
+        for quarter in range(2):
+            for out, block, fields in places:
+                if fields != [2]:
+                    project(out, fields, block, w1a, slice(quarter * P, (quarter + 1) * P))
+        for out, block, fields in places:
+            if fields == [2]:
+                project(out, fields, block, w1a)
         w2a_grouped = stage("w2a")
         interleave(nc.scalar.copy, w2a_grouped[:], w2_raw[0][:])
         w2a = quantise("w2a", flat(w2a_grouped), HALF)
         w1b_grouped = shared.tile([P, HALF, PACK], BF16, name="w1b_grouped", offset=1024, align_bytes=64)
-        interleave(nc.vector.tensor_copy, w1b_grouped[:], w1_raw[1][:])
-        left_a = early.tile([P, 3 * BLOCKS, PACK, P // 2], F32, name="left_a", offset=4096, align_bytes=64)
+        interleave(nc.vector.tensor_copy, w1b_grouped[:], w1_back[:])
+        left_a = early.tile([P, 3 * BLOCKS, PACK, P // 2], F32, name="left_a", offset=6144, align_bytes=64)
         for bank, places, slots in zip(left_a_banks, (slice(0, 2), slice(0, 2), slice(0, 1)), (slice(0, 2), slice(3, 5), slice(5, 6))):
             nc.scalar.copy(left_a[:, slots], bank[:, places, :].rearrange("p s (m j) -> p s j m", j=PACK))
         nc.vector.tensor_tensor(left_a[:, 2], dealt(left_a_banks[2][:, 1, :]), left_a[:, 0], ADD)

@@ -19,8 +19,11 @@ ADD = mybir.AluOpType.add
 P = 128
 PACK = 4
 QUADRANT = 32
+SCALE_ROWS = K // 32
+LIST_ROWS = 16
 HALF = H // 2
 BLOCKS = V // P
+TERMS = 3
 LINE = 4
 
 
@@ -31,6 +34,7 @@ def tile_picked_zfibi_none_po_kernel(
     with ExitStack() as ctx:
         keep = ctx.enter_context(tc.tile_pool(name="keep", bufs=1))
         shared = ctx.enter_context(tc.tile_pool(name="shared", bufs=1))
+        late = ctx.enter_context(tc.tile_pool(name="late", bufs=1))
         early = ctx.enter_context(tc.tile_pool(name="early", bufs=1))
         psum = ctx.enter_context(tc.psum_pool(name="psum", bufs=8))
 
@@ -43,14 +47,14 @@ def tile_picked_zfibi_none_po_kernel(
         nc.gpsimd.memset(warm_up[:, :8], 0.0)
         nc.scalar.copy(warm_up[:, 8:], warm_up[:, :8])
 
-        offsets = keep.tile([P, S // 16], U16, name="offsets")
+        offsets = keep.tile([P, S // LIST_ROWS], U16, name="offsets")
         scale_table = early.tile([P, T], U8, name="scale_table", offset=3072, align_bytes=64)
-        nc.vector.memset(scale_table[: P - 16, :].bitcast(I32), 0)
+        nc.vector.memset(scale_table[: P - SCALE_ROWS, :].bitcast(I32), 0)
         x_scale = keep.tile([P, S], U8, name="x_scale", align_bytes=64)
         nc.vector.memset(x_scale[:].bitcast(I32), 0)
         word_table = keep.tile([P, T], U32, name="word_table", align_bytes=64)
         words = x_words[0].rearrange("p n t -> p (n t)").bitcast(I32)
-        nc.sync.dma_start(scale_table[P - 16 :, :].bitcast(I32), x_scales[0].bitcast(I32))
+        nc.sync.dma_start(scale_table[P - SCALE_ROWS :, :].bitcast(I32), x_scales[0].bitcast(I32))
         nc.sync.dma_start(offsets[:], offs)
         w1_first = load(keep.tile([P, PACK, P], F32, name="w1_first", tag="w2_raw1", align_bytes=64), w1, 0, P)
         nc.sync.dma_start(word_table[:].bitcast(I32), words)
@@ -63,9 +67,6 @@ def tile_picked_zfibi_none_po_kernel(
                 grouped.rearrange("p (c i) j -> p c j i", i=LINE),
                 planes.rearrange("p j (c i) -> p c j i", i=LINE),
             )
-
-        def stage(tag):
-            return keep.tile([P, HALF, PACK], BF16, name="grouped", tag=tag, align_bytes=64)
 
         def flat(grouped):
             return grouped[:].rearrange("p c j -> p (c j)")
@@ -89,25 +90,28 @@ def tile_picked_zfibi_none_po_kernel(
 
         quantise_quarter(w1_first, 0, "w1_quarter0")
 
-        x_spread = keep.tile([P, S], U8, name="x_spread", tag="w3_raw", align_bytes=64)
+        x_spread = late.tile([P, S], U8, name="x_spread", offset=3584, align_bytes=64)
         nc.vector.tensor_copy(x_spread[:], scale_table[:].indirect(offsets[:]))
         for q in range(4):
             queue = nc.scalar if q % 2 else nc.sync
+            first_row = P - SCALE_ROWS + 4 * q
             queue.dma_start(
                 x_scale[QUADRANT * q : QUADRANT * q + 4, :].bitcast(I32),
-                x_spread[P - 16 + 4 * q : P - 12 + 4 * q, :].bitcast(I32),
+                x_spread[first_row : first_row + 4, :].bitcast(I32),
             )
         w1_second = load(early.tile([P, PACK, P], F32, name="w1_second", offset=4096, align_bytes=64), w1, 1, P)
         w2_raw = [load(early.tile([P, PACK, HALF], F32, name="w2_raw0", offset=6144, align_bytes=64), w2, 0)]
         w1_back = load(early.tile([P, PACK, HALF], F32, name="w1_back", offset=0, align_bytes=64), w1, 1)
         w2_raw.append(load(keep.tile([P, PACK, HALF], F32, name="w2_raw1", align_bytes=64), w2, 1))
-        w3_raw = keep.tile([P, PACK, N], F32, name="w3_raw", align_bytes=64)
-        nc.sync.dma_start(w3_raw[:], w3.rearrange("(p j) c -> p j c", j=PACK))
+        w3_raw = [
+            load(late.tile([P, PACK, HALF], F32, name=f"w3_raw{half}", offset=4096 * half, align_bytes=64), w3, half)
+            for half in range(2)
+        ]
         x_code = {}
 
         def gather(fields, tag):
             gathered = keep.tile([P, len(fields), V], U32, name="gathered", tag=tag, align_bytes=64)
-            columns = slice(fields[0] * V // 16, (fields[-1] + 1) * V // 16)
+            columns = slice(fields[0] * V // LIST_ROWS, (fields[-1] + 1) * V // LIST_ROWS)
             nc.vector.tensor_copy(
                 gathered[:].rearrange("p d v -> p (d v)"), word_table[:].indirect(offsets[:, columns])
             )
@@ -141,28 +145,18 @@ def tile_picked_zfibi_none_po_kernel(
                 banks.append(bank)
             return banks
 
-        def dealt(columns):
-            return columns.rearrange("p (m j) -> p j m", j=PACK)
-
-        def evict(tag, bank, places=slice(0, 2)):
-            left = keep.tile([P, 2, PACK, P // 2], F32, name="left", tag=tag, align_bytes=64)
-            nc.scalar.copy(left[:, places], bank[:, places, :].rearrange("p s (m j) -> p s j m", j=PACK))
-            return left
+        def by_slot(places):
+            return places.rearrange("p s (m j) -> p s j m", j=PACK)
 
         product = [keep.tile([P, BLOCKS, PACK, P], F32, name="product0", align_bytes=64)]
         low, high = slice(0, P // 2), slice(P // 2, P)
 
         def multiply(k, blocks, rows, right, left, slots=slice(0, PACK)):
-            nc.vector.tensor_tensor(
-                product[k][:, blocks, slots, rows],
-                right.rearrange("p s (m j) -> p s j m", j=PACK)[:, :, slots],
-                left[:, :, slots],
-                MULT,
-            )
+            nc.vector.tensor_tensor(product[k][:, blocks, slots, rows], by_slot(right)[:, :, slots], left[:, :, slots], MULT)
 
         left_fields = ([0], [0, 1], [2])
         right_fields = ([1], [2, 3], [3])
-        by_term = [[(0, k), (1, k)] for k in range(3)]
+        by_term = [[(0, k), (1, k)] for k in range(TERMS)]
         by_block = [[(0, 0), (0, 1)], [(0, 2), (1, 0)], [(1, 1), (1, 2)]]
 
         first_left = [[(0, [0]), (1, [0])], [(1, [0, 1]), (0, [2])], [(1, [2]), (0, [1])]]
@@ -175,51 +169,61 @@ def tile_picked_zfibi_none_po_kernel(
         for out, block, fields in places:
             if fields == [2]:
                 project(out, fields, block, w1a)
-        w2a_grouped = stage("w2a")
+        w2a_grouped = keep.tile([P, HALF, PACK], BF16, name="w2a_grouped", align_bytes=64)
         interleave(nc.scalar.copy, w2a_grouped[:], w2_raw[0][:])
         w2a = quantise("w2a", flat(w2a_grouped), HALF)
-        w1b_grouped = shared.tile([P, HALF, PACK], BF16, name="w1b_grouped", offset=1024, align_bytes=64)
+        w1b_grouped = shared.tile([P, HALF, PACK], BF16, name="w1b_grouped", offset=3072, align_bytes=64)
         interleave(nc.vector.tensor_copy, w1b_grouped[:], w1_back[:])
-        left_a = early.tile([P, 3 * BLOCKS, PACK, P // 2], F32, name="left_a", offset=6144, align_bytes=64)
-        for bank, places, slots in zip(left_a_banks, (slice(0, 2), slice(0, 2), slice(0, 1)), (slice(0, 2), slice(3, 5), slice(5, 6))):
-            nc.scalar.copy(left_a[:, slots], bank[:, places, :].rearrange("p s (m j) -> p s j m", j=PACK))
-        nc.vector.tensor_tensor(left_a[:, 2], dealt(left_a_banks[2][:, 1, :]), left_a[:, 0], ADD)
+        left_a = early.tile([P, TERMS * BLOCKS, PACK, P // 2], F32, name="left_a", offset=6144, align_bytes=64)
+
+        def evict_left_a(n, count, first):
+            nc.scalar.copy(left_a[:, first : first + count], by_slot(left_a_banks[n][:, :count, :]))
+
+        evict_left_a(0, 2, 0)
+        evict_left_a(1, 2, 3)
         w1b = quantise("w1b", flat(w1b_grouped), HALF)
+        nc.vector.tensor_tensor(left_a[:, 2:3], by_slot(left_a_banks[2][:, 1:, :]), left_a[:, 0:1], ADD)
         right_a = project_pairs([[(b, right_fields[k]) for b, k in pair] for pair in by_term], w2a)
         left_b_banks = project_pairs([[(b, left_fields[k]) for b, k in pair] for pair in by_block], w1b)
 
-        w2b_grouped = shared.tile([P, HALF, PACK], BF16, name="w2b_grouped", offset=1024, align_bytes=64)
+        w2b_grouped = shared.tile([P, HALF, PACK], BF16, name="w2b_grouped", offset=3072, align_bytes=64)
         interleave(nc.scalar.copy, w2b_grouped[:, :P, :], w2_raw[1][:, :, :P])
         nc.gpsimd.tensor_scalar(
             w2b_grouped[:, P:, :], w2_raw[1][:, :, P:].rearrange("p j c -> p c j"), 1.0, 0.0, MULT, ADD
         )
-        w2b = quantise("w2b", flat(w2b_grouped), HALF)
+        evict_left_a(2, 1, 5)
         product.append(keep.tile([P, BLOCKS, PACK, P], F32, name="product1", align_bytes=64))
-        product.append(shared.tile([P, BLOCKS, PACK, P], F32, name="product2", offset=2048, align_bytes=64))
-        for k in range(3):
+        for k in range(2):
             multiply(k, slice(0, BLOCKS), low, right_a[k][:], left_a[:, 2 * k : 2 * k + 2])
+        w2b = quantise("w2b", flat(w2b_grouped), HALF)
+        product.append(shared.tile([P, BLOCKS, PACK, P], F32, name="product2", offset=4096, align_bytes=64))
+        multiply(2, slice(0, BLOCKS), low, right_a[2][:], left_a[:, 4:6])
 
-        left_b = [evict(tag, bank) for tag, bank in zip(("w2_raw1", "left_b1", "left_b2"), left_b_banks)]
+        left_b = []
+        for tag, bank in zip(("w2_raw1", "left_b1", "left_b2"), left_b_banks):
+            left_b.append(keep.tile([P, 2, PACK, P // 2], F32, name="left_b", tag=tag, align_bytes=64))
+            nc.scalar.copy(left_b[-1][:], by_slot(bank[:]))
         right_b = project_pairs([[(b, right_fields[k]) for b, k in pair] for pair in by_block], w2b)
         for n, pair in enumerate(by_block):
             for place, (block, k) in enumerate(pair):
                 here = slice(place, place + 1)
-                for slots in ((slice(0, 2), slice(2, 4)) if (block, k) == (1, 2) else (slice(0, 4),)):
+                is_last = (block, k) == (BLOCKS - 1, TERMS - 1)
+                for slots in (slice(0, 2), slice(2, 4)) if is_last else (slice(0, 4),):
                     multiply(k, slice(block, block + 1), high, right_b[n][:, here, :], left_b[n][:, here], slots)
 
         w3_code = keep.tile([P, N], U32, name="w3_code", align_bytes=64)
         w3_scale = keep.tile([P, N], U8, name="w3_scale", align_bytes=64)
-        w3_read = w3_raw[:].rearrange("p j (m t) -> p t m j", t=PACK)
-        w3_front = shared.tile([P, 2, P, PACK], BF16, name="w3_front", offset=0, align_bytes=64)
-        nc.gpsimd.tensor_scalar(w3_front[:], w3_read[:, :2], 1.0, 0.0, MULT, ADD)
-        w3_back = keep.tile([P, 2, P, PACK], BF16, name="w3_back", tag="w2_raw1", align_bytes=64)
-        nc.scalar.copy(w3_back[:].rearrange("p t m j -> p m j t"), w3_read[:, 2:].rearrange("p t m j -> p m j t"))
-        for half, grouped in enumerate((w3_front, w3_back)):
+        w3_read = [raw[:].rearrange("p j (m t) -> p m t j", t=PACK) for raw in w3_raw]
+        w3_grouped = shared.tile([P, PACK, P, PACK], BF16, name="w3_grouped", offset=0, align_bytes=64)
+        w3_write = w3_grouped[:].rearrange("p t m j -> p m t j")
+        nc.gpsimd.tensor_scalar(w3_write[:, low], w3_read[0], 1.0, 0.0, MULT, ADD)
+        nc.scalar.copy(w3_write[:, high].rearrange("p m t j -> p m j t"), w3_read[1].rearrange("p m t j -> p m j t"))
+        for half in range(2):
             cols = slice(half * HALF, (half + 1) * HALF)
             nc.vector.quantize_mx(
                 out=w3_code[:, cols].bitcast(FP8X4),
                 scales=w3_scale[:, cols],
-                in_=grouped[:].rearrange("p t m j -> p (t m j)"),
+                in_=w3_grouped[:, 2 * half : 2 * half + 2].rearrange("p t m j -> p (t m j)"),
             )
 
         z_grouped = []
@@ -227,14 +231,14 @@ def tile_picked_zfibi_none_po_kernel(
             grouped = keep.tile([P, P, PACK], BF16, name=f"z_grouped{block}", align_bytes=64)
             for slots in ([0, 1, 2, 3],) if block == 0 else ([0, 1], [2, 3]):
                 z_bank = psum.tile([P, len(slots), P], F32, name="bank", tag="bank")
-                for k in range(3):
+                for k in range(TERMS):
                     for place, t in enumerate(slots):
                         nc.tensor.matmul(
                             z_bank[:, place, :],
                             product[k][:, block, t, :],
                             identity[:],
                             start=(k == 0 and place == 0),
-                            stop=(k == 2 and place == len(slots) - 1),
+                            stop=(k == TERMS - 1 and place == len(slots) - 1),
                             is_transpose=True,
                         )
                 nc.scalar.copy(grouped[:, :, slots[0] : slots[-1] + 1], z_bank[:].rearrange("p t v -> p v t"))
@@ -242,7 +246,7 @@ def tile_picked_zfibi_none_po_kernel(
 
         out_banks = []
         for block in range(BLOCKS):
-            z_code, z_scale = quantise(f"zq{block}", z_grouped[block][:].rearrange("p v t -> p (v t)"), P)
+            z_code, z_scale = quantise(f"zq{block}", flat(z_grouped[block]), P)
             for pair in range(2):
                 out_bank = psum.tile([P, 2, P], F32, name="bank", tag="bank")
                 for place in range(2):
@@ -289,4 +293,4 @@ def tile_picked_zfibi_none_po_kernel(
 
         for r in range(4):
             queue = nc.scalar if r % 2 else nc.sync
-            queue.dma_start(out_2[0, r:16:4, :].bitcast(I32), out_scale[r:P:QUADRANT, :].bitcast(I32))
+            queue.dma_start(out_2[0, r:SCALE_ROWS:4, :].bitcast(I32), out_scale[r:P:QUADRANT, :].bitcast(I32))

from contextlib import ExitStack

import concourse.mybir as mybir
from concourse.masks import make_identity

K, T, S, V, H, N = 512, 4096, 1024, 256, 512, 512
FLOPS = 7 * 2 * K * H * V

F32 = mybir.dt.float32
BF16 = mybir.dt.bfloat16
I32 = mybir.dt.int32
U32 = mybir.dt.uint32
U16 = mybir.dt.uint16
U8 = mybir.dt.uint8
FP8X4 = mybir.dt.float8_e4m3fn_x4
MULT = mybir.AluOpType.mult
ADD = mybir.AluOpType.add

P = 128
PACK = 4
QUADRANT = 32
SCALE_ROWS = K // 32
LIST_ROWS = 16
HALF = H // 2
BLOCKS = V // P
TERMS = 3
LINE = 4


def tile_picked_zfibi_none_po_kernel(
    tc, x_words, x_scales, w1, w2, w3, offs, out_0, out_1, out_2
):
    nc = tc.nc
    with ExitStack() as ctx:
        keep = ctx.enter_context(tc.tile_pool(name="keep", bufs=1))
        shared = ctx.enter_context(tc.tile_pool(name="shared", bufs=1))
        late = ctx.enter_context(tc.tile_pool(name="late", bufs=1))
        early = ctx.enter_context(tc.tile_pool(name="early", bufs=1))
        psum = ctx.enter_context(tc.psum_pool(name="psum", bufs=8))

        def load(raw, weight, part, width=HALF):
            rows = weight.rearrange("(p j) c -> p j c", j=PACK)
            nc.sync.dma_start(raw[:], rows[:, :, part * width : (part + 1) * width])
            return raw

        warm_up = keep.tile([P, 16], F32, name="warm_up")
        nc.gpsimd.memset(warm_up[:, :8], 0.0)
        nc.scalar.copy(warm_up[:, 8:], warm_up[:, :8])

        offsets = keep.tile([P, S // LIST_ROWS], U16, name="offsets")
        scale_table = early.tile([P, T], U8, name="scale_table", offset=3072, align_bytes=64)
        nc.vector.memset(scale_table[: P - SCALE_ROWS, :].bitcast(I32), 0)
        x_scale = keep.tile([P, S], U8, name="x_scale", align_bytes=64)
        nc.vector.memset(x_scale[:].bitcast(I32), 0)
        word_table = keep.tile([P, T], U32, name="word_table", align_bytes=64)
        words = x_words[0].rearrange("p n t -> p (n t)").bitcast(I32)
        nc.sync.dma_start(scale_table[P - SCALE_ROWS :, :].bitcast(I32), x_scales[0].bitcast(I32))
        nc.sync.dma_start(offsets[:], offs)
        w1_first = load(keep.tile([P, PACK, P], F32, name="w1_first", tag="w2_raw1", align_bytes=64), w1, 0, P)
        nc.sync.dma_start(word_table[:].bitcast(I32), words)

        identity = keep.tile([P, P], F32, name="identity", align_bytes=64)
        make_identity(nc, identity[:])

        def interleave(copy, grouped, planes):
            copy(
                grouped.rearrange("p (c i) j -> p c j i", i=LINE),
                planes.rearrange("p j (c i) -> p c j i", i=LINE),
            )

        def flat(grouped):
            return grouped[:].rearrange("p c j -> p (c j)")

        def quantise(name, grouped, width):
            codes = keep.tile([P, width], U32, name=name + "_code", align_bytes=64)
            scales = keep.tile([P, width], U8, name=name + "_scale", align_bytes=64)
            nc.vector.quantize_mx(out=codes[:].bitcast(FP8X4), scales=scales[:], in_=grouped)
            return codes, scales

        w1a = (
            keep.tile([P, HALF], U32, name="w1a_code", align_bytes=64),
            keep.tile([P, HALF], U8, name="w1a_scale", align_bytes=64),
        )

        def quantise_quarter(raw, part, tag):
            grouped = keep.tile([P, P, PACK], BF16, name="quarter", tag=tag, align_bytes=64)
            interleave(nc.scalar.copy, grouped[:], raw[:])
            cols = slice(part * P, (part + 1) * P)
            nc.vector.quantize_mx(out=w1a[0][:, cols].bitcast(FP8X4), scales=w1a[1][:, cols], in_=flat(grouped))

        quantise_quarter(w1_first, 0, "w1_quarter0")

        x_spread = late.tile([P, S], U8, name="x_spread", offset=3584, align_bytes=64)
        nc.vector.tensor_copy(x_spread[:], scale_table[:].indirect(offsets[:]))
        for q in range(4):
            queue = nc.scalar if q % 2 else nc.sync
            first_row = P - SCALE_ROWS + 4 * q
            queue.dma_start(
                x_scale[QUADRANT * q : QUADRANT * q + 4, :].bitcast(I32),
                x_spread[first_row : first_row + 4, :].bitcast(I32),
            )
        w1_second = load(early.tile([P, PACK, P], F32, name="w1_second", offset=4096, align_bytes=64), w1, 1, P)
        w2_raw = [load(early.tile([P, PACK, HALF], F32, name="w2_raw0", offset=6144, align_bytes=64), w2, 0)]
        w1_back = load(early.tile([P, PACK, HALF], F32, name="w1_back", offset=0, align_bytes=64), w1, 1)
        w2_raw.append(load(keep.tile([P, PACK, HALF], F32, name="w2_raw1", align_bytes=64), w2, 1))
        w3_raw = [
            load(late.tile([P, PACK, HALF], F32, name=f"w3_raw{half}", offset=4096 * half, align_bytes=64), w3, half)
            for half in range(2)
        ]
        x_code = {}

        def gather(fields, tag):
            gathered = keep.tile([P, len(fields), V], U32, name="gathered", tag=tag, align_bytes=64)
            columns = slice(fields[0] * V // LIST_ROWS, (fields[-1] + 1) * V // LIST_ROWS)
            nc.vector.tensor_copy(
                gathered[:].rearrange("p d v -> p (d v)"), word_table[:].indirect(offsets[:, columns])
            )
            for n, d in enumerate(fields):
                x_code[d] = gathered[:, n, :]

        gather([0, 1], "x_code01")
        gather([2], "x_code2")
        quantise_quarter(w1_second, 1, "x_code3")
        gather([3], "x_code3")

        def project(out, fields, block, weight, cols=slice(0, HALF)):
            for n, d in enumerate(fields):
                first = d * V + block * P
                nc.tensor.matmul_mx(
                    out=out[:, cols],
                    lhsT=x_code[d][:, block * P : (block + 1) * P].bitcast(FP8X4),
                    lhsT_scale=x_scale[:, first : first + P],
                    rhs=weight[0][:, cols].bitcast(FP8X4),
                    rhs_scale=weight[1][:, cols],
                    start=(n == 0),
                    stop=(n == len(fields) - 1),
                )

        def project_pairs(pairs, weight):
            banks = []
            for pair in pairs:
                bank = psum.tile([P, 2, HALF], F32, name="bank", tag="bank")
                for place, (block, fields) in enumerate(pair):
                    project(bank[:, place, :], fields, block, weight)
                banks.append(bank)
            return banks

        def by_slot(places):
            return places.rearrange("p s (m j) -> p s j m", j=PACK)

        product = [keep.tile([P, BLOCKS, PACK, P], F32, name="product0", align_bytes=64)]
        low, high = slice(0, P // 2), slice(P // 2, P)

        def multiply(k, blocks, rows, right, left, slots=slice(0, PACK)):
            nc.vector.tensor_tensor(product[k][:, blocks, slots, rows], by_slot(right)[:, :, slots], left[:, :, slots], MULT)

        left_fields = ([0], [0, 1], [2])
        right_fields = ([1], [2, 3], [3])
        by_term = [[(0, k), (1, k)] for k in range(TERMS)]
        by_block = [[(0, 0), (0, 1)], [(0, 2), (1, 0)], [(1, 1), (1, 2)]]

        first_left = [[(0, [0]), (1, [0])], [(1, [0, 1]), (0, [2])], [(1, [2]), (0, [1])]]
        left_a_banks = [psum.tile([P, 2, HALF], F32, name="bank", tag="bank") for pair in first_left]
        places = [(bank[:, n, :], *pair[n]) for bank, pair in zip(left_a_banks, first_left) for n in range(2)]
        for quarter in range(2):
            for out, block, fields in places:
                if fields != [2]:
                    project(out, fields, block, w1a, slice(quarter * P, (quarter + 1) * P))
        for out, block, fields in places:
            if fields == [2]:
                project(out, fields, block, w1a)
        w2a_grouped = keep.tile([P, HALF, PACK], BF16, name="w2a_grouped", align_bytes=64)
        interleave(nc.scalar.copy, w2a_grouped[:], w2_raw[0][:])
        w2a = quantise("w2a", flat(w2a_grouped), HALF)
        w1b_grouped = shared.tile([P, HALF, PACK], BF16, name="w1b_grouped", offset=3072, align_bytes=64)
        interleave(nc.vector.tensor_copy, w1b_grouped[:], w1_back[:])
        left_a = early.tile([P, TERMS * BLOCKS, PACK, P // 2], F32, name="left_a", offset=6144, align_bytes=64)

        def evict_left_a(n, count, first):
            nc.scalar.copy(left_a[:, first : first + count], by_slot(left_a_banks[n][:, :count, :]))

        evict_left_a(0, 2, 0)
        evict_left_a(1, 2, 3)
        w1b = quantise("w1b", flat(w1b_grouped), HALF)
        nc.vector.tensor_tensor(left_a[:, 2:3], by_slot(left_a_banks[2][:, 1:, :]), left_a[:, 0:1], ADD)
        right_a = project_pairs([[(b, right_fields[k]) for b, k in pair] for pair in by_term], w2a)
        left_b_banks = project_pairs([[(b, left_fields[k]) for b, k in pair] for pair in by_block], w1b)

        w2b_grouped = shared.tile([P, HALF, PACK], BF16, name="w2b_grouped", offset=3072, align_bytes=64)
        interleave(nc.scalar.copy, w2b_grouped[:, :P, :], w2_raw[1][:, :, :P])
        nc.gpsimd.tensor_scalar(
            w2b_grouped[:, P:, :], w2_raw[1][:, :, P:].rearrange("p j c -> p c j"), 1.0, 0.0, MULT, ADD
        )
        evict_left_a(2, 1, 5)
        product.append(keep.tile([P, BLOCKS, PACK, P], F32, name="product1", align_bytes=64))
        for k in range(2):
            multiply(k, slice(0, BLOCKS), low, right_a[k][:], left_a[:, 2 * k : 2 * k + 2])
        w2b = quantise("w2b", flat(w2b_grouped), HALF)
        product.append(shared.tile([P, BLOCKS, PACK, P], F32, name="product2", offset=4096, align_bytes=64))
        multiply(2, slice(0, BLOCKS), low, right_a[2][:], left_a[:, 4:6])

        left_b = []
        for tag, bank in zip(("w2_raw1", "left_b1", "left_b2"), left_b_banks):
            left_b.append(keep.tile([P, 2, PACK, P // 2], F32, name="left_b", tag=tag, align_bytes=64))
            nc.scalar.copy(left_b[-1][:], by_slot(bank[:]))
        right_b = project_pairs([[(b, right_fields[k]) for b, k in pair] for pair in by_block], w2b)
        for n, pair in enumerate(by_block):
            for place, (block, k) in enumerate(pair):
                here = slice(place, place + 1)
                is_last = (block, k) == (BLOCKS - 1, TERMS - 1)
                for slots in (slice(0, 2), slice(2, 4)) if is_last else (slice(0, 4),):
                    multiply(k, slice(block, block + 1), high, right_b[n][:, here, :], left_b[n][:, here], slots)

        w3_code = keep.tile([P, N], U32, name="w3_code", align_bytes=64)
        w3_scale = keep.tile([P, N], U8, name="w3_scale", align_bytes=64)
        w3_read = [raw[:].rearrange("p j (m t) -> p m t j", t=PACK) for raw in w3_raw]
        w3_grouped = shared.tile([P, PACK, P, PACK], BF16, name="w3_grouped", offset=0, align_bytes=64)
        w3_write = w3_grouped[:].rearrange("p t m j -> p m t j")
        nc.gpsimd.tensor_scalar(w3_write[:, low], w3_read[0], 1.0, 0.0, MULT, ADD)
        nc.scalar.copy(w3_write[:, high].rearrange("p m t j -> p m j t"), w3_read[1].rearrange("p m t j -> p m j t"))
        for half in range(2):
            cols = slice(half * HALF, (half + 1) * HALF)
            nc.vector.quantize_mx(
                out=w3_code[:, cols].bitcast(FP8X4),
                scales=w3_scale[:, cols],
                in_=w3_grouped[:, 2 * half : 2 * half + 2].rearrange("p t m j -> p (t m j)"),
            )

        z_grouped = []
        for block in range(BLOCKS):
            grouped = keep.tile([P, P, PACK], BF16, name=f"z_grouped{block}", align_bytes=64)
            for slots in ([0, 1, 2, 3],) if block == 0 else ([0, 1], [2, 3]):
                z_bank = psum.tile([P, len(slots), P], F32, name="bank", tag="bank")
                for k in range(TERMS):
                    for place, t in enumerate(slots):
                        nc.tensor.matmul(
                            z_bank[:, place, :],
                            product[k][:, block, t, :],
                            identity[:],
                            start=(k == 0 and place == 0),
                            stop=(k == TERMS - 1 and place == len(slots) - 1),
                            is_transpose=True,
                        )
                nc.scalar.copy(grouped[:, :, slots[0] : slots[-1] + 1], z_bank[:].rearrange("p t v -> p v t"))
            z_grouped.append(grouped)

        out_banks = []
        for block in range(BLOCKS):
            z_code, z_scale = quantise(f"zq{block}", flat(z_grouped[block]), P)
            for pair in range(2):
                out_bank = psum.tile([P, 2, P], F32, name="bank", tag="bank")
                for place in range(2):
                    t = 2 * pair + place
                    nc.tensor.matmul_mx(
                        out=out_bank[:, place, :],
                        lhsT=w3_code[:, t * P : (t + 1) * P].bitcast(FP8X4),
                        lhsT_scale=w3_scale[:, t * P : (t + 1) * P],
                        rhs=z_code[:].bitcast(FP8X4),
                        rhs_scale=z_scale[:],
                        start=True,
                        stop=True,
                    )
                out_banks.append(out_bank)

        out_code = keep.tile([P, V], U32, name="out_code", align_bytes=64)
        out_scale = keep.tile([P, V], U8, name="out_scale", align_bytes=64)
        out_words = out_1[0].rearrange("p n t -> p (n t)").bitcast(I32)
        out_rows = out_0.rearrange("(p t) v -> p t v", t=PACK)

        def quantise_out(grouped, first, width):
            nc.vector.quantize_mx(
                out=out_code[:, first : first + width].bitcast(FP8X4),
                scales=out_scale[:, first : first + width],
                in_=grouped.rearrange("p v t -> p (v t)"),
            )

        for block in range(BLOCKS):
            cols = slice(block * P, (block + 1) * P)
            result = keep.tile([P, PACK, P], F32, name=f"result{block}", align_bytes=64)
            out_grouped = keep.tile([P, P, PACK], BF16, name=f"out_grouped{block}", align_bytes=64)
            for pair in range(2):
                slots = slice(2 * pair, 2 * pair + 2)
                nc.scalar.copy(result[:, slots, :], out_banks[2 * block + pair][:])
                nc.sync.dma_start(out_rows[:, slots, cols], result[:, slots, :])
            if block == 0:
                interleave(nc.vector.tensor_copy, out_grouped[:], result[:])
                quantise_out(out_grouped[:], 0, P)
            else:
                for part, copy in ((low, nc.vector.tensor_copy), (high, nc.scalar.copy)):
                    interleave(copy, out_grouped[:, part, :], result[:, :, part])
                    quantise_out(out_grouped[:, part, :], P + part.start, P // 2)
        nc.sync.dma_start(out_words, out_code[:].bitcast(I32))

        for r in range(4):
            queue = nc.scalar if r % 2 else nc.sync
            queue.dma_start(out_2[0, r:SCALE_ROWS:4, :].bitcast(I32), out_scale[r:P:QUADRANT, :].bitcast(I32))
